import numpy as np
import ml_dtypes


def mxq(x, axis, fmt="e4m3"):
    dtype, down = {"e4m3": (ml_dtypes.float8_e4m3fn, 7), "e5m2": (ml_dtypes.float8_e5m2, 14)}[fmt]
    v = np.moveaxis(np.asarray(x, np.float32).astype(ml_dtypes.bfloat16).astype(np.float64), axis, -1)
    blocks = v.reshape(v.shape[:-1] + (-1, 32))
    amax = np.abs(blocks).max(-1, keepdims=True)
    byte = np.maximum(np.where(amax > 0, np.frexp(amax)[1] - 1 + 127, 0) - down, 1)
    scale = np.exp2(byte - 127.0)
    codes = (blocks / scale).astype(np.float32).astype(dtype).astype(np.float64)
    return np.moveaxis((codes * scale).reshape(v.shape), -1, axis)


WIDE = False


def mx_kscale(k):
    if not WIDE:
        return np.ones(k)
    levels = np.array([10, -10, 5, -5, 0])
    if k % 512:
        return np.exp2(np.random.permutation(np.resize(levels, k // 32))).repeat(32)
    a = np.empty((k // 512, 16))
    for p in range(k // 512):
        a[p, :8] = np.random.permutation(np.resize(levels, 8))
        for g in range(8):
            far = levels[np.abs(levels - a[p, g]) >= 10]
            a[p, g + 8] = far[np.random.randint(len(far))]
    return np.exp2(a.ravel()).repeat(32)


BF16 = ml_dtypes.bfloat16


def bf(x):
    return np.asarray(x, np.float32).astype(BF16)


def f64(x):
    return np.asarray(x).astype(np.float64)


E2M1 = np.array([0.0, 0.5, 1.0, 1.5, 2.0, 3.0, 4.0, 6.0, -0.0, -0.5, -1.0, -1.5, -2.0, -3.0, -4.0, -6.0])


def pack_weight(w, fmt):
    k, n = w.shape
    w = f64(bf(w)).reshape(k // 32, 32, n)
    amax = np.abs(w).max(1)
    if fmt == "e4m3":
        byte = np.frexp(amax)[1] - 1 + 127 - 7
    else:
        mant, ex = np.frexp(amax / 6.0)
        byte = np.where(mant > 0.5, ex, ex - 1) + 127
    byte = np.clip(np.where(amax > 0, byte, 1), 1, 254)
    scaled = (w * np.exp2(127.0 - byte)[:, None, :]).reshape(k, n).astype(np.float32)
    by_word = np.ascontiguousarray(scaled.reshape(k // 512, 128, 4, n).transpose(0, 1, 3, 2))
    if fmt == "e4m3":
        words = by_word.astype(ml_dtypes.float8_e4m3fn).view(np.uint8)
    else:
        c = by_word.astype(ml_dtypes.float4_e2m1fn).view(np.uint8) & 0xF
        words = c[..., 0::2] | (c[..., 1::2] << 4)
    return np.ascontiguousarray(words), np.ascontiguousarray(byte.astype(np.uint8).reshape(k // 512, 16, n))


def unpack_weight(words, scales, fmt):
    g, p, n, _ = words.shape
    if fmt == "e4m3":
        vals = np.ascontiguousarray(words).view(ml_dtypes.float8_e4m3fn).astype(np.float64)
    else:
        nib = np.empty((g, p, n, 4), np.uint8)
        nib[..., 0::2] = words & 0xF
        nib[..., 1::2] = words >> 4
        vals = E2M1[nib]
    vals = vals * np.repeat(np.exp2(scales.astype(np.float64) - 127.0), 8, axis=1)[..., None]
    return vals.transpose(0, 1, 3, 2).reshape(g * 512, n)
def pack4(w):
    words, scales = pack_weight(w, "e2m1")
    return words.reshape(words.shape[0], 128, -1), scales


def unpack4(words, scales):
    return unpack_weight(words.reshape(words.shape[0], 128, -1, 2), scales, "e2m1")


def planes(Y):
    n, m = Y.shape
    b = f64(bf(Y)).reshape(n // 32, 32, m)
    amax = np.abs(b).max(1)
    byte = np.clip(np.where(amax > 0, np.frexp(amax)[1] - 1 + 127 - 7, 1), 1, 254)
    codes = (b * np.exp2(127.0 - byte)[:, None, :]).reshape(n, m).astype(np.float32).astype(ml_dtypes.float8_e4m3fn).view(np.uint8)
    words = codes.reshape(n // 512, 128, 4, m).transpose(0, 1, 3, 2)
    return np.ascontiguousarray(words), np.ascontiguousarray(byte.astype(np.uint8).reshape(n // 512, 16, m))


B, N, C, E = 2, 1024, 512, 512


def predicted_prior(xq, wq, b):
    return 1.0 / (1.0 + np.exp(-((xq @ wq) + b)))


def aggregate(weights, vq):
    return (mxq(weights, 2, "e4m3") @ vq) / np.sqrt(vq.shape[1])


def setup_inputs():
    s, t = mx_kscale(C), mx_kscale(N)
    x = bf(np.random.standard_normal((B, N, C)) * s)
    w_words, w_scales = pack4(np.random.standard_normal((C, N)) * 1.5 / np.sqrt(C) / s[:, None])
    return {"x": x,
            "w_words": w_words,
            "w_scales": w_scales,
            "b": bf(0.5 * np.random.standard_normal(N)),
            "g": bf(np.random.standard_normal(N) * t),
            "v": bf(np.random.standard_normal((B, N, E)) / t[:, None])}


def core(x, w_words, w_scales, b, g, v):
    p = predicted_prior(mxq(f64(x), 2, "e4m3"), unpack4(w_words, w_scales), f64(b))
    g = f64(g)
    pi = p * g
    pe = (1.0 - p) * g
    vq = mxq(f64(v), 1, "e4m3")
    yi = aggregate(pi, vq)
    ye = aggregate(pe, vq)
    return np.concatenate([yi, ye], axis=-1)


def reference(x, w_words, w_scales, b, g, v):
    R_out = core(x, w_words, w_scales, b, g, v)
    words, scales = planes(np.moveaxis(R_out, 1, 0).reshape(1024, -1))
    return R_out, words, scales

@@ -1,0 +1,402 @@
+from contextlib import ExitStack
+
+import concourse.mybir as mybir
+from concourse.masks import make_identity
+
+F32 = mybir.dt.float32
+BF16 = mybir.dt.bfloat16
+U32 = mybir.dt.uint32
+I32 = mybir.dt.int32
+U8 = mybir.dt.uint8
+FP8X4 = mybir.dt.float8_e4m3fn_x4
+FP4X4 = mybir.dt.float4_e2m1fn_x4
+ALU = mybir.AluOpType
+ACT = mybir.ActivationFunctionType
+
+B, N, C, E = 2, 1024, 512, 512
+P = 128
+FLOPS = 2 * B * N * N * C + 2 * 2 * B * N * N * E
+
+
+def tile_contextpriorintrainteraggregation_x2_kernel(
+    tc, x, w_words, w_scales, b, g, v, out_0, out_1, out_2
+):
+    nc = tc.nc
+    with ExitStack() as ctx:
+        keep = ctx.enter_context(tc.tile_pool(name="keep", bufs=1))
+        raws = ctx.enter_context(tc.tile_pool(name="raws", bufs=4))
+        grouped = ctx.enter_context(tc.tile_pool(name="grouped", bufs=2))
+        priors = ctx.enter_context(tc.tile_pool(name="priors", bufs=4))
+        gated = ctx.enter_context(tc.tile_pool(name="gated", bufs=3))
+        codes = ctx.enter_context(tc.tile_pool(name="codes", bufs=6))
+        results = ctx.enter_context(tc.tile_pool(name="results", bufs=4))
+        regroup = ctx.enter_context(tc.tile_pool(name="regroup", bufs=3))
+        zbanks = ctx.enter_context(tc.psum_pool(name="zbanks", bufs=4))
+        ybanks = ctx.enter_context(tc.psum_pool(name="ybanks", bufs=4))
+
+        w_raw = keep.tile([P, 2 * N], U8, name="w_raw", align_bytes=64)
+        ws_raw = keep.tile([P, N], U8, name="ws_raw", align_bytes=64)
+        w_codes = [keep.tile([P, 4, P, 2], U8, name="w_codes%d" % i, align_bytes=64) for i in range(2)]
+        w_plane = [keep.tile([P, 4, P], U8, name="w_plane%d" % i, align_bytes=64) for i in range(2)]
+        b_raw = keep.tile([P, 2, 4], BF16, name="b_raw")
+        g_raw = keep.tile([P, 2, 4], BF16, name="g_raw")
+        b_col = keep.tile([P, 8], F32, name="b_col")
+        g_col = keep.tile([P, 8], F32, name="g_col")
+        ng_col = keep.tile([P, 8], F32, name="ng_col")
+        ident = keep.tile([P, P], F32, name="ident")
+        warm = keep.tile([P, 1], F32, name="warm")
+        warm2 = keep.tile([P, 1], F32, name="warm2")
+        x_codes = [keep.tile([P, 512], U32, name="x_codes%d" % i, align_bytes=64) for i in range(4)]
+        x_plane = [keep.tile([P, 512], U8, name="x_plane%d" % i, align_bytes=64) for i in range(4)]
+        v_codes = [keep.tile([P, 512], U32, name="v_codes%d" % i, align_bytes=64) for i in range(4)]
+        v_plane = [keep.tile([P, 512], U8, name="v_plane%d" % i, align_bytes=64) for i in range(4)]
+        y_codes = keep.tile([P, 2, 2 * N], U32, name="y_codes", align_bytes=64)
+        y_plane = keep.tile([P, 2, 2 * N], U8, name="y_plane", align_bytes=64)
+
+        x_tiles = {}
+        v_tiles = {}
+        x_groups = {}
+        v_groups = {}
+        p_tiles = {}
+        z_tiles = {}
+        gated_tiles = {}
+        code_tiles = {}
+        y_tiles = {}
+        result_tiles = {}
+        regrouped = {}
+
+        def load_x(sb, half):
+            n, gp = divmod(sb, 2)
+            src = x[n, 512 * gp : 512 * gp + 512, :].rearrange("(p t) k -> p t k", t=4)
+            if half == 0:
+                x_raw = raws.tile([P, 4, C], BF16, name="x_raw")
+                x_tiles[sb] = x_raw
+            nc.sync.dma_start(
+                out=x_tiles[sb][:, 2 * half : 2 * half + 2, :], in_=src[:, 2 * half : 2 * half + 2, :]
+            )
+
+        def load_v(n, jg):
+            v_raw = raws.tile([P, 4, E], BF16, name="v_raw")
+            v_tiles[n, jg] = v_raw
+            nc.sync.dma_start(
+                out=v_raw[:], in_=v[n, 512 * jg : 512 * jg + 512, :].rearrange("(p s) e -> p s e", s=4)
+            )
+
+        def permute_w(jg):
+            nc.vector.tensor_copy(
+                out=w_codes[jg][:],
+                in_=w_raw[:, 1024 * jg : 1024 * jg + 1024].rearrange("p (m s b) -> p s m b", s=4, b=2),
+            )
+            nc.vector.tensor_copy(
+                out=w_plane[jg][:],
+                in_=ws_raw[:, 512 * jg : 512 * jg + 512].rearrange("p (m s) -> p s m", s=4),
+            )
+
+        def turn_x(sb, half):
+            words = x_tiles[sb][:].rearrange("p t k -> p (t k)").bitcast(F32)
+            turned = zbanks.tile([P, 2, 2, P], F32, name="turned", tag="z")
+            z_tiles["x", sb, half] = turned
+            for i in range(2):
+                t = 2 * half + i
+                for u in range(2):
+                    nc.tensor.transpose(turned[:, i, u, :], words[:, 256 * t + u : 256 * t + 256 : 2], ident[:])
+
+        def copy_x(sb, half, engine):
+            if half == 0:
+                x_group = grouped.tile([P, 512, 4], BF16, name="x_group", align_bytes=64)
+                x_groups[sb] = x_group
+            dst = x_groups[sb][:].rearrange("p c j -> p (c j)").bitcast(F32)
+            dst = dst[:, 512 * half : 512 * half + 512].rearrange("p (t r u) -> p t r u", t=2, u=2)
+            src = z_tiles.pop(("x", sb, half))[:].rearrange("p t u r -> p t r u")
+            if engine == "S":
+                nc.scalar.copy(out=dst, in_=src)
+            else:
+                nc.vector.tensor_copy(out=dst, in_=src)
+
+        def quant_x(sb):
+            nc.vector.quantize_mx(
+                out=x_codes[sb][:].bitcast(FP8X4),
+                scales=x_plane[sb][:],
+                in_=x_groups.pop(sb)[:].rearrange("p c j -> p (c j)"),
+            )
+
+        def group_v(n, jg, engine):
+            v_group = grouped.tile([P, 512, 4], BF16, name="v_group", align_bytes=64)
+            v_groups[n, jg] = v_group
+            dst = v_group[:].rearrange("p (c i) s -> p c s i", i=4)
+            src = v_tiles.pop((n, jg))[:].rearrange("p s (c i) -> p c s i", i=4)
+            if engine == "S":
+                nc.scalar.copy(out=dst, in_=src)
+            else:
+                nc.vector.tensor_copy(out=dst, in_=src)
+
+        def quant_v(n, jg):
+            nc.vector.quantize_mx(
+                out=v_codes[2 * n + jg][:].bitcast(FP8X4),
+                scales=v_plane[2 * n + jg][:],
+                in_=v_groups.pop((n, jg))[:].rearrange("p c s -> p (c s)"),
+            )
+
+        def logits(q):
+            k, s = divmod(q, 4)
+            sb, jg = divmod(k, 2)
+            z = zbanks.tile([P, 512], F32, name="z", tag="z")
+            z_tiles[q] = z
+            nc.tensor.matmul_mx(
+                out=z[:],
+                lhsT=w_codes[jg][:].rearrange("p s m b -> p (s m b)")[:, 256 * s : 256 * s + 256].bitcast(FP4X4),
+                lhsT_scale=w_plane[jg][:, s, :],
+                rhs=x_codes[sb][:].bitcast(FP8X4),
+                rhs_scale=x_plane[sb][:],
+                start=True,
+                stop=True,
+            )
+
+        def sigmoid(q):
+            k, s = divmod(q, 4)
+            jg = k % 2
+            if s == 0:
+                prior = priors.tile([P, 4, 512], F32, name="prior")
+                p_tiles[k] = prior
+            nc.scalar.activation(
+                out=p_tiles[k][:, s, :],
+                in_=z_tiles.pop(q)[:],
+                func=ACT.Sigmoid,
+                bias=b_col[:, 4 * jg + s : 4 * jg + s + 1],
+                scale=1.0,
+            )
+
+        def gate(sb, h, jg):
+            k = 2 * sb + jg
+            gate_out = gated.tile([P, 512, 4], BF16, name="gate_out", align_bytes=64)
+            gated_tiles[sb, h, jg] = gate_out
+            if h == 0:
+                nc.vector.tensor_tensor(
+                    out=gate_out[:].rearrange("p (c i) s -> p c s i", i=4),
+                    in0=p_tiles[k][:].rearrange("p s (c i) -> p c s i", i=4),
+                    in1=g_col[:, 4 * jg : 4 * jg + 4].unsqueeze(1).unsqueeze(3).to_broadcast([P, 128, 4, 4]),
+                    op=ALU.mult,
+                )
+            else:
+                nc.vector.scalar_tensor_tensor(
+                    out=gate_out[:],
+                    in0=p_tiles[k][:].rearrange("p s c -> p c s"),
+                    scalar=1.0,
+                    in1=ng_col[:, 4 * jg : 4 * jg + 4].unsqueeze(1).to_broadcast([P, 512, 4]),
+                    op0=ALU.subtract,
+                    op1=ALU.mult,
+                )
+
+        def quant_gated(sb, h, jg):
+            g_codes = codes.tile([P, 512], U32, name="g_codes", align_bytes=64)
+            g_plane = codes.tile([P, 512], U8, name="g_plane", align_bytes=64)
+            code_tiles[sb, h, jg] = (g_codes, g_plane)
+            nc.vector.quantize_mx(
+                out=g_codes[:].bitcast(FP8X4),
+                scales=g_plane[:],
+                in_=gated_tiles.pop((sb, h, jg))[:].rearrange("p c s -> p (c s)"),
+            )
+
+        def aggregate_pass(sb, h, t, jg):
+            n = sb // 2
+            if jg == 0:
+                y = ybanks.tile([P, 512], F32, name="y", tag="y")
+                y_tiles[sb, h, t] = y
+            g_codes, g_plane = code_tiles[sb, h, jg]
+            nc.tensor.matmul_mx(
+                out=y_tiles[sb, h, t][:],
+                lhsT=g_codes[:, 128 * t : 128 * t + 128].bitcast(FP8X4),
+                lhsT_scale=g_plane[:, 128 * t : 128 * t + 128],
+                rhs=v_codes[2 * n + jg][:].bitcast(FP8X4),
+                rhs_scale=v_plane[2 * n + jg][:],
+                start=(jg == 0),
+                stop=(jg == 1),
+            )
+
+        def scale_y(sb, h, t, engine):
+            if (sb, h) not in result_tiles:
+                result = results.tile([P, 4, 512], F32, name="result")
+                result_tiles[sb, h] = result
+            dst = result_tiles[sb, h][:, t, :]
+            src = y_tiles.pop((sb, h, t))[:]
+            if engine == "S":
+                nc.scalar.activation(out=dst, in_=src, func=ACT.Copy, scale=1.0 / 32.0)
+            else:
+                nc.vector.tensor_scalar(out=dst, in0=src, scalar1=1.0 / 32.0, scalar2=None, op0=ALU.mult)
+
+        def store_y(sb, h):
+            n, gp = divmod(sb, 2)
+            dst = out_0[n, 512 * gp : 512 * gp + 512, 512 * h : 512 * h + 512].rearrange("(p t) e -> p t e", t=4)
+            nc.sync.dma_start(out=dst, in_=result_tiles[sb, h][:])
+
+        def regroup_y(sb, h, engine, e0=0, e1=512):
+            if (sb, h) not in regrouped:
+                y_group = regroup.tile([P, 512, 4], BF16, name="y_group", align_bytes=64)
+                regrouped[sb, h] = y_group
+            dst = regrouped[sb, h][:, e0:e1, :].rearrange("p (c i) t -> p c t i", i=4)
+            src = result_tiles[sb, h][:, :, e0:e1].rearrange("p t (c i) -> p c t i", i=4)
+            if engine == "S":
+                nc.scalar.copy(out=dst, in_=src)
+            else:
+                nc.vector.tensor_copy(out=dst, in_=src)
+
+        def quant_y(sb, h, e0=0, e1=512):
+            n, gp = divmod(sb, 2)
+            m0 = 1024 * n + 512 * h
+            nc.vector.quantize_mx(
+                out=y_codes[:, gp, m0 + e0 : m0 + e1].bitcast(FP8X4),
+                scales=y_plane[:, gp, m0 + e0 : m0 + e1],
+                in_=regrouped[sb, h][:, e0:e1, :].rearrange("p c t -> p (c t)"),
+            )
+
+        def store_codes(sb, h):
+            n, gp = divmod(sb, 2)
+            m0 = 1024 * n + 512 * h
+            nc.sync.dma_start(
+                out=out_1[gp].rearrange("p m t -> p (m t)")[:, 4 * m0 : 4 * m0 + 2048].bitcast(I32),
+                in_=y_codes[:, gp, m0 : m0 + 512].bitcast(I32),
+            )
+
+        def store_scales(sb, h, width):
+            n, gp = divmod(sb, 2)
+            m0 = 1024 * n + 512 * h
+            for quad in range(4):
+                nc.sync.dma_start(
+                    out=out_2[gp, 4 * quad : 4 * quad + 4, m0 : m0 + width].bitcast(I32),
+                    in_=y_plane[32 * quad : 32 * quad + 4, gp, m0 : m0 + width].bitcast(I32),
+                )
+
+        with tc.manual_schedule():
+            nc.vector.memset(ws_raw[:].bitcast(I32), 0)
+            nc.gpsimd.memset(warm[:], 0.0)
+            make_identity(nc, ident[:])
+            nc.scalar.activation(out=warm2[:], in_=warm[:], func=ACT.Sigmoid)
+
+            nc.sync.dma_start(out=w_raw[:].bitcast(I32), in_=w_words[0].bitcast(I32))
+            load_x(0, 0)
+            load_x(0, 1)
+            nc.scalar.dma_start(out=b_raw[:], in_=b.rearrange("(j p s) -> p j s", j=2, s=4))
+            nc.scalar.dma_start(out=g_raw[:], in_=g.rearrange("(j p s) -> p j s", j=2, s=4))
+            for quad in range(4):
+                nc.scalar.dma_start(
+                    out=ws_raw[32 * quad : 32 * quad + 4, :].bitcast(I32),
+                    in_=w_scales[0, 4 * quad : 4 * quad + 4, :].bitcast(I32),
+                )
+            load_v(0, 0)
+            load_x(1, 0)
+            load_x(1, 1)
+            load_v(0, 1)
+            for sb in (2, 3):
+                load_x(sb, 0)
+                load_x(sb, 1)
+            load_v(1, 0)
+            load_v(1, 1)
+            bv = b_raw[:].rearrange("p j s -> p (j s)")
+            gv = g_raw[:].rearrange("p j s -> p (j s)")
+            nc.gpsimd.tensor_scalar(out=b_col[:], in0=bv, scalar1=1.0, scalar2=0.0, op0=ALU.mult, op1=ALU.add)
+            nc.gpsimd.tensor_scalar(out=g_col[:], in0=gv, scalar1=1.0, scalar2=0.0, op0=ALU.mult, op1=ALU.add)
+            nc.gpsimd.tensor_scalar(out=ng_col[:], in0=gv, scalar1=-1.0, scalar2=0.0, op0=ALU.mult, op1=ALU.add)
+
+            turn_x(0, 0)
+            turn_x(0, 1)
+            permute_w(0)
+            copy_x(0, 0, "S")
+            copy_x(0, 1, "V")
+            quant_x(0)
+            for q in range(4):
+                logits(q)
+                sigmoid(q)
+            permute_w(1)
+            turn_x(1, 0)
+            turn_x(1, 1)
+            copy_x(1, 0, "S")
+            copy_x(1, 1, "S")
+            for q in range(4, 8):
+                logits(q)
+                sigmoid(q)
+            group_v(0, 0, "V")
+
+            def order(m):
+                sb, r = divmod(m, 4)
+                return sb, r // 2, r % 2
+
+            for m in range(16):
+                sb, r = divmod(m, 4)
+                gate(*order(m))
+                if m == 0:
+                    quant_x(1)
+                    logits(8)
+                    logits(9)
+                else:
+                    quant_gated(*order(m - 1))
+                for q in (2 * m + 10, 2 * m + 11):
+                    if q < 32:
+                        logits(q)
+                if r == 0 and sb in (0, 1):
+                    turn_x(sb + 2, 0)
+                    turn_x(sb + 2, 1)
+                if r == 2:
+                    for t in range(4):
+                        for jg in range(2):
+                            aggregate_pass(sb, 0, t, jg)
+                if r == 0 and sb > 0:
+                    for t in range(4):
+                        for jg in range(2):
+                            aggregate_pass(sb - 1, 1, t, jg)
+                if r == 3:
+                    for t in range(4):
+                        scale_y(sb, 0, t, "S")
+                    store_y(sb, 0)
+                if r == 1 and sb > 0:
+                    for t in range(4):
+                        scale_y(sb - 1, 1, t, "S")
+                    store_y(sb - 1, 1)
+                for q in (2 * m + 8, 2 * m + 9):
+                    if q < 32:
+                        sigmoid(q)
+                if r == 1 and sb in (0, 1):
+                    copy_x(sb + 2, 0, "S")
+                    copy_x(sb + 2, 1, "S")
+                if m == 1:
+                    group_v(1, 0, "S")
+                if m == 2:
+                    group_v(1, 1, "S")
+                if r == 0 and sb > 0:
+                    regroup_y(sb - 1, 0, "V" if sb == 2 else "S")
+                if r == 2 and sb > 0:
+                    regroup_y(sb - 1, 1, "S")
+                if m == 0:
+                    quant_v(0, 0)
+                    group_v(0, 1, "V")
+                if m == 1:
+                    quant_v(0, 1)
+                if r == 2 and sb in (0, 1):
+                    quant_x(sb + 2)
+                if m == 3:
+                    quant_v(1, 0)
+                if m == 4:
+                    quant_v(1, 1)
+                if r == 1 and sb > 0:
+                    quant_y(sb - 1, 0)
+                    store_codes(sb - 1, 0)
+                if r == 3 and sb > 0:
+                    quant_y(sb - 1, 1)
+                    store_codes(sb - 1, 1)
+                    store_scales(sb - 1, 0, 1024)
+
+            quant_gated(*order(15))
+            for t in range(4):
+                aggregate_pass(3, 1, t, 0)
+            for t in range(4):
+                aggregate_pass(3, 1, t, 1)
+            regroup_y(3, 0, "V")
+            quant_y(3, 0)
+            store_codes(3, 0)
+            for t in range(4):
+                scale_y(3, 1, t, "SV"[t % 2])
+            store_y(3, 1)
+            regroup_y(3, 1, "S", 0, 128)
+            regroup_y(3, 1, "V", 128, 512)
+            quant_y(3, 1)
+            store_codes(3, 1)
+            store_scales(3, 0, 1024)

@@ -15,6 +15,7 @@ ACT = mybir.ActivationFunctionType
 
 B, N, C, E = 2, 1024, 512, 512
 P = 128
+CFG = {"gv": ["S", "S", "S", "S"], "t5": ["V", "S", "V", "S", "S", "S", "V"], "yc": ["S", "V", "V", "S"], "cut": 256}
 FLOPS = 2 * B * N * N * C + 2 * 2 * B * N * N * E
 
 
@@ -42,7 +43,6 @@ def tile_contextpriorintrainteraggregation_x2_kernel(
         g_raw = keep.tile([P, 2, 4], BF16, name="g_raw")
         b_col = keep.tile([P, 8], F32, name="b_col")
         g_col = keep.tile([P, 8], F32, name="g_col")
-        ng_col = keep.tile([P, 8], F32, name="ng_col")
         ident = keep.tile([P, P], F32, name="ident")
         warm = keep.tile([P, 1], F32, name="warm")
         warm2 = keep.tile([P, 1], F32, name="warm2")
@@ -65,15 +65,14 @@ def tile_contextpriorintrainteraggregation_x2_kernel(
         result_tiles = {}
         regrouped = {}
 
-        def load_x(sb, half):
+        def load_x(sb, halves):
             n, gp = divmod(sb, 2)
-            src = x[n, 512 * gp : 512 * gp + 512, :].rearrange("(p t) k -> p t k", t=4)
-            if half == 0:
-                x_raw = raws.tile([P, 4, C], BF16, name="x_raw")
-                x_tiles[sb] = x_raw
-            nc.sync.dma_start(
-                out=x_tiles[sb][:, 2 * half : 2 * half + 2, :], in_=src[:, 2 * half : 2 * half + 2, :]
-            )
+            rows = x[n, 512 * gp : 512 * gp + 512, :].rearrange("(p t) k -> p t k", t=4)
+            x_raw = raws.tile([P, 4, C], BF16, name="x_raw")
+            x_tiles[sb] = x_raw
+            for half in halves:
+                lo, hi = half
+                nc.sync.dma_start(out=x_raw[:, lo:hi, :], in_=rows[:, lo:hi, :])
 
         def load_v(n, jg):
             v_raw = raws.tile([P, 4, E], BF16, name="v_raw")
@@ -87,44 +86,45 @@ def tile_contextpriorintrainteraggregation_x2_kernel(
                 out=w_codes[jg][:],
                 in_=w_raw[:, 1024 * jg : 1024 * jg + 1024].rearrange("p (m s b) -> p s m b", s=4, b=2),
             )
+
+        def permute_ws(jg):
             nc.vector.tensor_copy(
                 out=w_plane[jg][:],
                 in_=ws_raw[:, 512 * jg : 512 * jg + 512].rearrange("p (m s) -> p s m", s=4),
             )
 
         def turn_x(sb, half):
-            words = x_tiles[sb][:].rearrange("p t k -> p (t k)").bitcast(F32)
             turned = zbanks.tile([P, 2, 2, P], F32, name="turned", tag="z")
             z_tiles["x", sb, half] = turned
             for i in range(2):
-                t = 2 * half + i
+                words = x_tiles[sb][:, 2 * half + i, :].bitcast(F32)
                 for u in range(2):
-                    nc.tensor.transpose(turned[:, i, u, :], words[:, 256 * t + u : 256 * t + 256 : 2], ident[:])
+                    nc.tensor.transpose(turned[:, i, u, :], words[:, u : 256 : 2], ident[:])
 
         def copy_x(sb, half, engine):
             if half == 0:
                 x_group = grouped.tile([P, 512, 4], BF16, name="x_group", align_bytes=64)
                 x_groups[sb] = x_group
-            dst = x_groups[sb][:].rearrange("p c j -> p (c j)").bitcast(F32)
-            dst = dst[:, 512 * half : 512 * half + 512].rearrange("p (t r u) -> p t r u", t=2, u=2)
-            src = z_tiles.pop(("x", sb, half))[:].rearrange("p t u r -> p t r u")
+            dst = x_groups[sb][:, 256 * half : 256 * half + 256, :].rearrange("p c j -> p (c j)").bitcast(F32)
+            dst = dst.rearrange("p (t r u) -> p t r u", t=2, u=2)
+            src = z_tiles["x", sb, half][:].rearrange("p t u r -> p t r u")
             if engine == "S":
                 nc.scalar.copy(out=dst, in_=src)
             else:
                 nc.vector.tensor_copy(out=dst, in_=src)
 
-        def quant_x(sb):
+        def quant_x(sb, c0=0, c1=512):
             nc.vector.quantize_mx(
-                out=x_codes[sb][:].bitcast(FP8X4),
-                scales=x_plane[sb][:],
-                in_=x_groups.pop(sb)[:].rearrange("p c j -> p (c j)"),
+                out=x_codes[sb][:, c0:c1].bitcast(FP8X4),
+                scales=x_plane[sb][:, c0:c1],
+                in_=x_groups[sb][:, c0:c1, :].rearrange("p c j -> p (c j)"),
             )
 
         def group_v(n, jg, engine):
             v_group = grouped.tile([P, 512, 4], BF16, name="v_group", align_bytes=64)
             v_groups[n, jg] = v_group
             dst = v_group[:].rearrange("p (c i) s -> p c s i", i=4)
-            src = v_tiles.pop((n, jg))[:].rearrange("p s (c i) -> p c s i", i=4)
+            src = v_tiles[n, jg][:].rearrange("p s (c i) -> p c s i", i=4)
             if engine == "S":
                 nc.scalar.copy(out=dst, in_=src)
             else:
@@ -134,67 +134,87 @@ def tile_contextpriorintrainteraggregation_x2_kernel(
             nc.vector.quantize_mx(
                 out=v_codes[2 * n + jg][:].bitcast(FP8X4),
                 scales=v_plane[2 * n + jg][:],
-                in_=v_groups.pop((n, jg))[:].rearrange("p c s -> p (c s)"),
+                in_=v_groups[n, jg][:].rearrange("p c s -> p (c s)"),
             )
 
-        def logits(q):
+        def logits(q, c0=0, c1=512):
             k, s = divmod(q, 4)
             sb, jg = divmod(k, 2)
-            z = zbanks.tile([P, 512], F32, name="z", tag="z")
-            z_tiles[q] = z
+            if c1 - c0 == 512 or s % 2 == 0:
+                z = zbanks.tile([P, 512], F32, name="z", tag="z")
+                z_tiles[q, c0] = z
+                lo = 0
+            else:
+                z = z_tiles[q - 1, c0]
+                z_tiles[q, c0] = z
+                lo = 256
             nc.tensor.matmul_mx(
-                out=z[:],
+                out=z[:, lo : lo + c1 - c0],
                 lhsT=w_codes[jg][:].rearrange("p s m b -> p (s m b)")[:, 256 * s : 256 * s + 256].bitcast(FP4X4),
                 lhsT_scale=w_plane[jg][:, s, :],
-                rhs=x_codes[sb][:].bitcast(FP8X4),
-                rhs_scale=x_plane[sb][:],
+                rhs=x_codes[sb][:, c0:c1].bitcast(FP8X4),
+                rhs_scale=x_plane[sb][:, c0:c1],
                 start=True,
                 stop=True,
             )
 
-        def sigmoid(q):
+        def sigmoid(q, c0=0, c1=512):
             k, s = divmod(q, 4)
             jg = k % 2
-            if s == 0:
+            if s == 0 and c0 == 0:
                 prior = priors.tile([P, 4, 512], F32, name="prior")
                 p_tiles[k] = prior
+            lo = 256 * (s % 2) if c1 - c0 == 256 else 0
             nc.scalar.activation(
-                out=p_tiles[k][:, s, :],
-                in_=z_tiles.pop(q)[:],
+                out=p_tiles[k][:, s, c0:c1],
+                in_=z_tiles[q, c0][:, lo : lo + c1 - c0],
                 func=ACT.Sigmoid,
                 bias=b_col[:, 4 * jg + s : 4 * jg + s + 1],
                 scale=1.0,
             )
 
-        def gate(sb, h, jg):
-            k = 2 * sb + jg
-            gate_out = gated.tile([P, 512, 4], BF16, name="gate_out", align_bytes=64)
-            gated_tiles[sb, h, jg] = gate_out
-            if h == 0:
-                nc.vector.tensor_tensor(
-                    out=gate_out[:].rearrange("p (c i) s -> p c s i", i=4),
-                    in0=p_tiles[k][:].rearrange("p s (c i) -> p c s i", i=4),
-                    in1=g_col[:, 4 * jg : 4 * jg + 4].unsqueeze(1).unsqueeze(3).to_broadcast([P, 128, 4, 4]),
-                    op=ALU.mult,
-                )
-            else:
-                nc.vector.scalar_tensor_tensor(
-                    out=gate_out[:],
-                    in0=p_tiles[k][:].rearrange("p s c -> p c s"),
-                    scalar=1.0,
-                    in1=ng_col[:, 4 * jg : 4 * jg + 4].unsqueeze(1).to_broadcast([P, 512, 4]),
-                    op0=ALU.subtract,
-                    op1=ALU.mult,
+        def gate(k, c0=0, c1=512):
+            jg = k % 2
+            for s in range(4):
+                pg = p_tiles[k][:, s, c0:c1]
+                nc.vector.tensor_scalar(
+                    out=pg, in0=pg, scalar1=g_col[:, 4 * jg + s : 4 * jg + s + 1], scalar2=None, op0=ALU.mult
                 )
 
-        def quant_gated(sb, h, jg):
+        def gated_tile(k, h, c0):
+            if c0 == 0:
+                gate_out = gated.tile([P, 512, 4], BF16, name="gate_out", align_bytes=64)
+                gated_tiles[k, h] = gate_out
+            return gated_tiles[k, h]
+
+        def inner(k, c0=0, c1=512, engine="V"):
+            dst = gated_tile(k, 0, c0)[:, c0:c1, :].rearrange("p (c i) s -> p c s i", i=4)
+            src = p_tiles[k][:, :, c0:c1].rearrange("p s (c i) -> p c s i", i=4)
+            if engine == "S":
+                nc.scalar.copy(out=dst, in_=src)
+            else:
+                nc.vector.tensor_copy(out=dst, in_=src)
+
+        def outer(k, c0=0, c1=512):
+            jg = k % 2
+            nc.vector.tensor_tensor(
+                out=gated_tile(k, 1, c0)[:, c0:c1, :].rearrange("p (c i) s -> p c s i", i=4),
+                in0=g_col[:, 4 * jg : 4 * jg + 4]
+                .unsqueeze(1)
+                .unsqueeze(3)
+                .to_broadcast([P, (c1 - c0) // 4, 4, 4]),
+                in1=p_tiles[k][:, :, c0:c1].rearrange("p s (c i) -> p c s i", i=4),
+                op=ALU.subtract,
+            )
+
+        def quant_gated(k, h):
             g_codes = codes.tile([P, 512], U32, name="g_codes", align_bytes=64)
             g_plane = codes.tile([P, 512], U8, name="g_plane", align_bytes=64)
-            code_tiles[sb, h, jg] = (g_codes, g_plane)
+            code_tiles[k // 2, h, k % 2] = (g_codes, g_plane)
             nc.vector.quantize_mx(
                 out=g_codes[:].bitcast(FP8X4),
                 scales=g_plane[:],
-                in_=gated_tiles.pop((sb, h, jg))[:].rearrange("p c s -> p (c s)"),
+                in_=gated_tiles[k, h][:].rearrange("p c s -> p (c s)"),
             )
 
         def aggregate_pass(sb, h, t, jg):
@@ -218,7 +238,7 @@ def tile_contextpriorintrainteraggregation_x2_kernel(
                 result = results.tile([P, 4, 512], F32, name="result")
                 result_tiles[sb, h] = result
             dst = result_tiles[sb, h][:, t, :]
-            src = y_tiles.pop((sb, h, t))[:]
+            src = y_tiles[sb, h, t][:]
             if engine == "S":
                 nc.scalar.activation(out=dst, in_=src, func=ACT.Copy, scale=1.0 / 32.0)
             else:
@@ -230,6 +250,10 @@ def tile_contextpriorintrainteraggregation_x2_kernel(
             nc.sync.dma_start(out=dst, in_=result_tiles[sb, h][:])
 
         def regroup_y(sb, h, engine, e0=0, e1=512):
+            if engine == "X":
+                regroup_y(sb, h, "S", 0, CFG["cut"])
+                regroup_y(sb, h, "V", CFG["cut"], 512)
+                return
             if (sb, h) not in regrouped:
                 y_group = regroup.tile([P, 512, 4], BF16, name="y_group", align_bytes=64)
                 regrouped[sb, h] = y_group
@@ -266,137 +290,181 @@ def tile_contextpriorintrainteraggregation_x2_kernel(
                     in_=y_plane[32 * quad : 32 * quad + 4, gp, m0 : m0 + width].bitcast(I32),
                 )
 
+        def turn_and(sb, half):
+            turn_x(sb, half)
+
         with tc.manual_schedule():
             nc.vector.memset(ws_raw[:].bitcast(I32), 0)
-            nc.gpsimd.memset(warm[:], 0.0)
             make_identity(nc, ident[:])
+            nc.gpsimd.memset(warm[:], 0.0)
             nc.scalar.activation(out=warm2[:], in_=warm[:], func=ACT.Sigmoid)
-
-            nc.sync.dma_start(out=w_raw[:].bitcast(I32), in_=w_words[0].bitcast(I32))
-            load_x(0, 0)
-            load_x(0, 1)
-            nc.scalar.dma_start(out=b_raw[:], in_=b.rearrange("(j p s) -> p j s", j=2, s=4))
-            nc.scalar.dma_start(out=g_raw[:], in_=g.rearrange("(j p s) -> p j s", j=2, s=4))
             for quad in range(4):
                 nc.scalar.dma_start(
                     out=ws_raw[32 * quad : 32 * quad + 4, :].bitcast(I32),
                     in_=w_scales[0, 4 * quad : 4 * quad + 4, :].bitcast(I32),
                 )
+            nc.scalar.dma_start(out=b_raw[:], in_=b.rearrange("(j p s) -> p j s", j=2, s=4))
+            nc.scalar.dma_start(out=g_raw[:], in_=g.rearrange("(j p s) -> p j s", j=2, s=4))
+            for jg in range(2):
+                nc.sync.dma_start(
+                    out=w_raw[:, 1024 * jg : 1024 * jg + 1024].bitcast(I32),
+                    in_=w_words[0, :, 1024 * jg : 1024 * jg + 1024].bitcast(I32),
+                )
+            load_x(0, ((0, 2), (2, 4)))
             load_v(0, 0)
-            load_x(1, 0)
-            load_x(1, 1)
+            load_x(1, ((0, 4),))
             load_v(0, 1)
-            for sb in (2, 3):
-                load_x(sb, 0)
-                load_x(sb, 1)
+            load_x(2, ((0, 4),))
+            load_x(3, ((0, 4),))
             load_v(1, 0)
             load_v(1, 1)
             bv = b_raw[:].rearrange("p j s -> p (j s)")
             gv = g_raw[:].rearrange("p j s -> p (j s)")
             nc.gpsimd.tensor_scalar(out=b_col[:], in0=bv, scalar1=1.0, scalar2=0.0, op0=ALU.mult, op1=ALU.add)
             nc.gpsimd.tensor_scalar(out=g_col[:], in0=gv, scalar1=1.0, scalar2=0.0, op0=ALU.mult, op1=ALU.add)
-            nc.gpsimd.tensor_scalar(out=ng_col[:], in0=gv, scalar1=-1.0, scalar2=0.0, op0=ALU.mult, op1=ALU.add)
 
             turn_x(0, 0)
             turn_x(0, 1)
-            permute_w(0)
             copy_x(0, 0, "S")
-            copy_x(0, 1, "V")
-            quant_x(0)
-            for q in range(4):
+            permute_w(0)
+            permute_ws(0)
+            quant_x(0, 0, 256)
+            copy_x(0, 1, "S")
+            permute_w(1)
+            quant_x(0, 256, 512)
+            for c0 in (0, 256):
+                for q in range(4):
+                    logits(q, c0, c0 + 256)
+                for q in range(4):
+                    sigmoid(q, c0, c0 + 256)
+            gate(0, 0, 256)
+            permute_ws(1)
+            for q in range(4, 8):
                 logits(q)
                 sigmoid(q)
-            permute_w(1)
             turn_x(1, 0)
             turn_x(1, 1)
             copy_x(1, 0, "S")
             copy_x(1, 1, "S")
-            for q in range(4, 8):
+            group_v(0, 0, CFG["gv"][0])
+            inner(0, 0, 256)
+            gate(0, 256, 512)
+            outer(0, 0, 256)
+            inner(0, 256, 512)
+            outer(0, 256, 512)
+            quant_gated(0, 0)
+            quant_x(1)
+
+            for q in range(8, 12):
                 logits(q)
-                sigmoid(q)
-            group_v(0, 0, "V")
-
-            def order(m):
-                sb, r = divmod(m, 4)
-                return sb, r // 2, r % 2
-
-            for m in range(16):
-                sb, r = divmod(m, 4)
-                gate(*order(m))
-                if m == 0:
-                    quant_x(1)
-                    logits(8)
-                    logits(9)
-                else:
-                    quant_gated(*order(m - 1))
-                for q in (2 * m + 10, 2 * m + 11):
-                    if q < 32:
-                        logits(q)
-                if r == 0 and sb in (0, 1):
-                    turn_x(sb + 2, 0)
-                    turn_x(sb + 2, 1)
-                if r == 2:
+            for k in range(1, 6):
+                sb, jg = divmod(k, 2)
+                gate(k)
+                quant_gated(k - 1, 1)
+                if jg == 0:
                     for t in range(4):
-                        for jg in range(2):
-                            aggregate_pass(sb, 0, t, jg)
-                if r == 0 and sb > 0:
+                        scale_y(sb - 1, 0, t, "S")
+                    store_y(sb - 1, 0)
+                for q in range(4 * k + 4, 4 * k + 8):
+                    sigmoid(q)
+                if k == 1:
+                    group_v(0, 1, CFG["gv"][1])
+                    quant_v(0, 0)
+                if jg == 0:
                     for t in range(4):
-                        for jg in range(2):
-                            aggregate_pass(sb - 1, 1, t, jg)
-                if r == 3:
-                    for t in range(4):
-                        scale_y(sb, 0, t, "S")
-                    store_y(sb, 0)
-                if r == 1 and sb > 0:
-                    for t in range(4):
+                        for j in range(2):
+                            aggregate_pass(sb - 1, 1, t, j)
                         scale_y(sb - 1, 1, t, "S")
                     store_y(sb - 1, 1)
-                for q in (2 * m + 8, 2 * m + 9):
-                    if q < 32:
-                        sigmoid(q)
-                if r == 1 and sb in (0, 1):
+                if k in (1, 3):
+                    turn_x(sb + 2, 0)
+                    turn_x(sb + 2, 1)
                     copy_x(sb + 2, 0, "S")
                     copy_x(sb + 2, 1, "S")
-                if m == 1:
-                    group_v(1, 0, "S")
-                if m == 2:
-                    group_v(1, 1, "S")
-                if r == 0 and sb > 0:
-                    regroup_y(sb - 1, 0, "V" if sb == 2 else "S")
-                if r == 2 and sb > 0:
-                    regroup_y(sb - 1, 1, "S")
-                if m == 0:
-                    quant_v(0, 0)
-                    group_v(0, 1, "V")
-                if m == 1:
+                if k in (3, 5):
+                    regroup_y(sb - 1, 0, CFG["t5"][2 * sb - 2])
+                    if CFG["t5"][2 * sb - 1] != "V":
+                        regroup_y(sb - 1, 1, CFG["t5"][2 * sb - 1])
+                inner(k)
+                if k in (3, 4):
+                    group_v(1, k - 3, CFG["gv"][k - 1])
+                if k in (3, 5) and CFG["t5"][2 * sb - 1] == "V":
+                    regroup_y(sb - 1, 1, "V")
+                if k == 4:
+                    quant_y(0, 1)
+                    store_codes(0, 1)
+                    store_scales(0, 0, 1024)
+                outer(k)
+                quant_gated(k, 0)
+                if k == 1:
                     quant_v(0, 1)
-                if r == 2 and sb in (0, 1):
-                    quant_x(sb + 2)
-                if m == 3:
-                    quant_v(1, 0)
-                if m == 4:
-                    quant_v(1, 1)
-                if r == 1 and sb > 0:
+                if k in (2, 4):
+                    quant_x(sb + 1)
+                if k in (4, 5):
+                    quant_v(1, k - 4)
+                if k in (3, 5):
                     quant_y(sb - 1, 0)
                     store_codes(sb - 1, 0)
-                if r == 3 and sb > 0:
-                    quant_y(sb - 1, 1)
-                    store_codes(sb - 1, 1)
-                    store_scales(sb - 1, 0, 1024)
+                for q in range(4 * k + 8, 4 * k + 12):
+                    logits(q)
+                if jg == 1:
+                    for t in range(4):
+                        for j in range(2):
+                            aggregate_pass(sb, 0, t, j)
 
-            quant_gated(*order(15))
+            gate(6)
+            quant_gated(5, 1)
+            for q in range(28, 32):
+                sigmoid(q)
+            for t in range(4):
+                scale_y(2, 0, t, "S")
+            store_y(2, 0)
+            for t in range(4):
+                for j in range(2):
+                    aggregate_pass(2, 1, t, j)
+                scale_y(2, 1, t, "S")
+            store_y(2, 1)
+            if CFG["t5"][4] != "V":
+                regroup_y(2, 0, CFG["t5"][4])
+            inner(6)
+            gate(7)
+            quant_gated(6, 0)
+            inner(7)
+            if CFG["t5"][4] == "V":
+                regroup_y(2, 0, "V")
+            quant_y(1, 1)
+            store_codes(1, 1)
+            store_scales(1, 0, 1024)
+            quant_gated(7, 0)
+            outer(6)
+            for t in range(4):
+                for j in range(2):
+                    aggregate_pass(3, 0, t, j)
+                scale_y(3, 0, t, "S")
+            store_y(3, 0)
+            if CFG["t5"][5] != "V":
+                regroup_y(2, 1, CFG["t5"][5])
+            outer(7)
+            quant_gated(6, 1)
+            if CFG["t5"][5] == "V":
+                regroup_y(2, 1, "V")
+            quant_gated(7, 1)
             for t in range(4):
                 aggregate_pass(3, 1, t, 0)
             for t in range(4):
                 aggregate_pass(3, 1, t, 1)
-            regroup_y(3, 0, "V")
+            regroup_y(3, 0, CFG["t5"][6])
+            quant_y(2, 0)
+            store_codes(2, 0)
+            for t in range(4):
+                scale_y(3, 1, t, CFG["yc"][t])
+            store_y(3, 1)
+            quant_y(2, 1)
+            store_codes(2, 1)
+            store_scales(2, 0, 1024)
             quant_y(3, 0)
             store_codes(3, 0)
-            for t in range(4):
-                scale_y(3, 1, t, "SV"[t % 2])
-            store_y(3, 1)
-            regroup_y(3, 1, "S", 0, 128)
-            regroup_y(3, 1, "V", 128, 512)
+            regroup_y(3, 1, "X")
             quant_y(3, 1)
             store_codes(3, 1)
             store_scales(3, 0, 1024)

@@ -15,7 +15,7 @@ ACT = mybir.ActivationFunctionType
 
 B, N, C, E = 2, 1024, 512, 512
 P = 128
-CFG = {"gv": ["S", "S", "S", "S"], "t5": ["V", "S", "V", "S", "S", "S", "V"], "yc": ["S", "V", "V", "S"], "cut": 256}
+CFG = {("v", 1, 0): "G", ("v", 1, 1): "G", ("y", 0, 0): "G", ("y", 0, 1): "G", ("y", 1, 0): "G", ("y", 1, 1): "G", ("y", 2, 0): "G", ("y", 2, 1): "S", ("y", 3, 0): "S", "innerS": [], "yc": ["S", "V", "V", "S"], "cut": 256}
 FLOPS = 2 * B * N * N * C + 2 * 2 * B * N * N * E
 
 
@@ -31,18 +31,21 @@ def tile_contextpriorintrainteraggregation_x2_kernel(
         gated = ctx.enter_context(tc.tile_pool(name="gated", bufs=3))
         codes = ctx.enter_context(tc.tile_pool(name="codes", bufs=6))
         results = ctx.enter_context(tc.tile_pool(name="results", bufs=4))
-        regroup = ctx.enter_context(tc.tile_pool(name="regroup", bufs=3))
+        regroups = ctx.enter_context(tc.tile_pool(name="regroups", bufs=2))
+        vgroups = ctx.enter_context(tc.tile_pool(name="vgroups", bufs=1))
+        ggroups = ctx.enter_context(tc.tile_pool(name="ggroups", bufs=1))
         zbanks = ctx.enter_context(tc.psum_pool(name="zbanks", bufs=4))
-        ybanks = ctx.enter_context(tc.psum_pool(name="ybanks", bufs=4))
+        ybanks = ctx.enter_context(tc.psum_pool(name="ybanks", bufs=3))
+        cbank = ctx.enter_context(tc.psum_pool(name="cbank", bufs=1))
 
         w_raw = keep.tile([P, 2 * N], U8, name="w_raw", align_bytes=64)
         ws_raw = keep.tile([P, N], U8, name="ws_raw", align_bytes=64)
         w_codes = [keep.tile([P, 4, P, 2], U8, name="w_codes%d" % i, align_bytes=64) for i in range(2)]
         w_plane = [keep.tile([P, 4, P], U8, name="w_plane%d" % i, align_bytes=64) for i in range(2)]
-        b_raw = keep.tile([P, 2, 4], BF16, name="b_raw")
-        g_raw = keep.tile([P, 2, 4], BF16, name="g_raw")
-        b_col = keep.tile([P, 8], F32, name="b_col")
-        g_col = keep.tile([P, 8], F32, name="g_col")
+        bg_rows = keep.tile([P, N], BF16, name="bg_rows", align_bytes=64)
+        bg_col = keep.tile([P, 16], F32, name="bg_col")
+        bg_bank = cbank.tile([P, 16 + P], BF16, name="bg_bank")
+        ident_b = keep.tile([P, P], BF16, name="ident_b")
         ident = keep.tile([P, P], F32, name="ident")
         warm = keep.tile([P, 1], F32, name="warm")
         warm2 = keep.tile([P, 1], F32, name="warm2")
@@ -63,7 +66,7 @@ def tile_contextpriorintrainteraggregation_x2_kernel(
         code_tiles = {}
         y_tiles = {}
         result_tiles = {}
-        regrouped = {}
+        y_groups = {}
 
         def load_x(sb, halves):
             n, gp = divmod(sb, 2)
@@ -120,21 +123,29 @@ def tile_contextpriorintrainteraggregation_x2_kernel(
                 in_=x_groups[sb][:, c0:c1, :].rearrange("p c j -> p (c j)"),
             )
 
-        def group_v(n, jg, engine):
-            v_group = grouped.tile([P, 512, 4], BF16, name="v_group", align_bytes=64)
-            v_groups[n, jg] = v_group
-            dst = v_group[:].rearrange("p (c i) s -> p c s i", i=4)
-            src = v_tiles[n, jg][:].rearrange("p s (c i) -> p c s i", i=4)
+        def group_v(n, jg, engine, e0=0, e1=512, held=False):
+            pool, what = (ggroups, "part_g") if engine == "G" or held else (grouped, "v_part%d" % (e1 - e0))
+            v_part = pool.tile([P, e1 - e0, 4], BF16, name=what, align_bytes=64)
+            v_groups[n, jg, e0] = v_part
+            regroup(v_part[:], v_tiles[n, jg][:, :, e0:e1], engine)
+
+        def regroup(part, rows, engine):
+            dst = part.rearrange("p (c i) t -> p c t i", i=4)
+            src = rows.rearrange("p t (c i) -> p c t i", i=4)
             if engine == "S":
                 nc.scalar.copy(out=dst, in_=src)
-            else:
+            elif engine == "V":
                 nc.vector.tensor_copy(out=dst, in_=src)
+            else:
+                nc.gpsimd.tensor_scalar(
+                    out=part, in0=rows.rearrange("p t c -> p c t"), scalar1=1.0, scalar2=0.0, op0=ALU.mult, op1=ALU.add
+                )
 
-        def quant_v(n, jg):
+        def quant_v(n, jg, e0=0, e1=512, base=0):
             nc.vector.quantize_mx(
-                out=v_codes[2 * n + jg][:].bitcast(FP8X4),
-                scales=v_plane[2 * n + jg][:],
-                in_=v_groups[n, jg][:].rearrange("p c s -> p (c s)"),
+                out=v_codes[2 * n + jg][:, e0:e1].bitcast(FP8X4),
+                scales=v_plane[2 * n + jg][:, e0:e1],
+                in_=v_groups[n, jg, base][:, e0 - base : e1 - base, :].rearrange("p c s -> p (c s)"),
             )
 
         def logits(q, c0=0, c1=512):
@@ -169,7 +180,7 @@ def tile_contextpriorintrainteraggregation_x2_kernel(
                 out=p_tiles[k][:, s, c0:c1],
                 in_=z_tiles[q, c0][:, lo : lo + c1 - c0],
                 func=ACT.Sigmoid,
-                bias=b_col[:, 4 * jg + s : 4 * jg + s + 1],
+                bias=bg_col[:, 8 * jg + 2 * s : 8 * jg + 2 * s + 1],
                 scale=1.0,
             )
 
@@ -178,7 +189,7 @@ def tile_contextpriorintrainteraggregation_x2_kernel(
             for s in range(4):
                 pg = p_tiles[k][:, s, c0:c1]
                 nc.vector.tensor_scalar(
-                    out=pg, in0=pg, scalar1=g_col[:, 4 * jg + s : 4 * jg + s + 1], scalar2=None, op0=ALU.mult
+                    out=pg, in0=pg, scalar1=bg_col[:, 8 * jg + 2 * s + 1 : 8 * jg + 2 * s + 2], scalar2=None, op0=ALU.mult
                 )
 
         def gated_tile(k, h, c0):
@@ -199,7 +210,7 @@ def tile_contextpriorintrainteraggregation_x2_kernel(
             jg = k % 2
             nc.vector.tensor_tensor(
                 out=gated_tile(k, 1, c0)[:, c0:c1, :].rearrange("p (c i) s -> p c s i", i=4),
-                in0=g_col[:, 4 * jg : 4 * jg + 4]
+                in0=bg_bank[:, 8 * jg + 1 : 8 * jg + 8 : 2]
                 .unsqueeze(1)
                 .unsqueeze(3)
                 .to_broadcast([P, (c1 - c0) // 4, 4, 4]),
@@ -250,27 +261,18 @@ def tile_contextpriorintrainteraggregation_x2_kernel(
             nc.sync.dma_start(out=dst, in_=result_tiles[sb, h][:])
 
         def regroup_y(sb, h, engine, e0=0, e1=512):
-            if engine == "X":
-                regroup_y(sb, h, "S", 0, CFG["cut"])
-                regroup_y(sb, h, "V", CFG["cut"], 512)
-                return
-            if (sb, h) not in regrouped:
-                y_group = regroup.tile([P, 512, 4], BF16, name="y_group", align_bytes=64)
-                regrouped[sb, h] = y_group
-            dst = regrouped[sb, h][:, e0:e1, :].rearrange("p (c i) t -> p c t i", i=4)
-            src = result_tiles[sb, h][:, :, e0:e1].rearrange("p t (c i) -> p c t i", i=4)
-            if engine == "S":
-                nc.scalar.copy(out=dst, in_=src)
-            else:
-                nc.vector.tensor_copy(out=dst, in_=src)
+            pool, what = (ggroups, "part_g") if engine == "G" else (regroups, "y_part%d" % (e1 - e0))
+            y_part = pool.tile([P, e1 - e0, 4], BF16, name=what, align_bytes=64)
+            y_groups[sb, h, e0] = y_part
+            regroup(y_part[:], result_tiles[sb, h][:, :, e0:e1], engine)
 
-        def quant_y(sb, h, e0=0, e1=512):
+        def quant_y(sb, h, e0=0, e1=512, base=0):
             n, gp = divmod(sb, 2)
             m0 = 1024 * n + 512 * h
             nc.vector.quantize_mx(
                 out=y_codes[:, gp, m0 + e0 : m0 + e1].bitcast(FP8X4),
                 scales=y_plane[:, gp, m0 + e0 : m0 + e1],
-                in_=regrouped[sb, h][:, e0:e1, :].rearrange("p c t -> p (c t)"),
+                in_=y_groups[sb, h, base][:, e0 - base : e1 - base, :].rearrange("p c t -> p (c t)"),
             )
 
         def store_codes(sb, h):
@@ -290,21 +292,52 @@ def tile_contextpriorintrainteraggregation_x2_kernel(
                     in_=y_plane[32 * quad : 32 * quad + 4, gp, m0 : m0 + width].bitcast(I32),
                 )
 
-        def turn_and(sb, half):
-            turn_x(sb, half)
+        GC = 384
+
+        def unit_early(u):
+            kind, a, d = u
+            f = group_v if kind == "v" else regroup_y
+            if CFG[u] == "S":
+                f(a, d, "S")
+            elif CFG[u] == "G":
+                f(a, d, "S", GC, 512)
+
+        def unit_main(u):
+            kind, a, d = u
+            f = group_v if kind == "v" else regroup_y
+            if CFG[u] == "V":
+                f(a, d, "V")
+            elif CFG[u] == "G":
+                f(a, d, "G", 0, GC)
+
+        def unit_quant(u):
+            kind, a, d = u
+            f = quant_v if kind == "v" else quant_y
+            if CFG[u] in ("G", "T"):
+                f(a, d, 0, 256, 0)
+                f(a, d, 256, GC, 0)
+                f(a, d, GC, 512, GC)
+            else:
+                f(a, d)
+            if kind == "y":
+                store_codes(a, d)
+                if d == 1:
+                    store_scales(a, 0, 1024)
 
         with tc.manual_schedule():
-            nc.vector.memset(ws_raw[:].bitcast(I32), 0)
+            nc.vector.memset(bg_rows[:].bitcast(I32), 0)
+            nc.gpsimd.memset(ws_raw[:].bitcast(I32), 0)
+            make_identity(nc, ident_b[:])
             make_identity(nc, ident[:])
             nc.gpsimd.memset(warm[:], 0.0)
-            nc.scalar.activation(out=warm2[:], in_=warm[:], func=ACT.Sigmoid)
+            nc.scalar.dma_start(out=bg_rows[0:1, :], in_=b.unsqueeze(0))
+            nc.scalar.dma_start(out=bg_rows[1:2, :], in_=g.unsqueeze(0))
             for quad in range(4):
                 nc.scalar.dma_start(
                     out=ws_raw[32 * quad : 32 * quad + 4, :].bitcast(I32),
                     in_=w_scales[0, 4 * quad : 4 * quad + 4, :].bitcast(I32),
                 )
-            nc.scalar.dma_start(out=b_raw[:], in_=b.rearrange("(j p s) -> p j s", j=2, s=4))
-            nc.scalar.dma_start(out=g_raw[:], in_=g.rearrange("(j p s) -> p j s", j=2, s=4))
+            nc.scalar.activation(out=warm2[:], in_=warm[:], func=ACT.Sigmoid)
             for jg in range(2):
                 nc.sync.dma_start(
                     out=w_raw[:, 1024 * jg : 1024 * jg + 1024].bitcast(I32),
@@ -318,14 +351,16 @@ def tile_contextpriorintrainteraggregation_x2_kernel(
             load_x(3, ((0, 4),))
             load_v(1, 0)
             load_v(1, 1)
-            bv = b_raw[:].rearrange("p j s -> p (j s)")
-            gv = g_raw[:].rearrange("p j s -> p (j s)")
-            nc.gpsimd.tensor_scalar(out=b_col[:], in0=bv, scalar1=1.0, scalar2=0.0, op0=ALU.mult, op1=ALU.add)
-            nc.gpsimd.tensor_scalar(out=g_col[:], in0=gv, scalar1=1.0, scalar2=0.0, op0=ALU.mult, op1=ALU.add)
 
             turn_x(0, 0)
+            for i in range(8):
+                jg, s = divmod(i, 4)
+                nc.tensor.transpose(
+                    bg_bank[:, 2 * i : 2 * i + P], bg_rows[:, 512 * jg + s : 512 * jg + 512 : 4], ident_b[:]
+                )
             turn_x(0, 1)
             copy_x(0, 0, "S")
+            nc.scalar.copy(out=bg_col[:], in_=bg_bank[:, 0:16])
             permute_w(0)
             permute_ws(0)
             quant_x(0, 0, 256)
@@ -346,15 +381,16 @@ def tile_contextpriorintrainteraggregation_x2_kernel(
             turn_x(1, 1)
             copy_x(1, 0, "S")
             copy_x(1, 1, "S")
-            group_v(0, 0, CFG["gv"][0])
+            group_v(0, 0, "S")
             inner(0, 0, 256)
             gate(0, 256, 512)
-            outer(0, 0, 256)
             inner(0, 256, 512)
+            outer(0, 0, 256)
             outer(0, 256, 512)
             quant_gated(0, 0)
             quant_x(1)
 
+            queue = [("v", 1, 0), ("v", 1, 1), ("y", 0, 0), ("y", 0, 1), ("y", 1, 0)]
             for q in range(8, 12):
                 logits(q)
             for k in range(1, 6):
@@ -365,11 +401,12 @@ def tile_contextpriorintrainteraggregation_x2_kernel(
                     for t in range(4):
                         scale_y(sb - 1, 0, t, "S")
                     store_y(sb - 1, 0)
+                if k == 1:
+                    group_v(0, 1, "S", 0, GC, True)
+                    group_v(0, 1, "S", GC, 512)
+                    quant_v(0, 0)
                 for q in range(4 * k + 4, 4 * k + 8):
                     sigmoid(q)
-                if k == 1:
-                    group_v(0, 1, CFG["gv"][1])
-                    quant_v(0, 0)
                 if jg == 0:
                     for t in range(4):
                         for j in range(2):
@@ -381,30 +418,20 @@ def tile_contextpriorintrainteraggregation_x2_kernel(
                     turn_x(sb + 2, 1)
                     copy_x(sb + 2, 0, "S")
                     copy_x(sb + 2, 1, "S")
-                if k in (3, 5):
-                    regroup_y(sb - 1, 0, CFG["t5"][2 * sb - 2])
-                    if CFG["t5"][2 * sb - 1] != "V":
-                        regroup_y(sb - 1, 1, CFG["t5"][2 * sb - 1])
-                inner(k)
-                if k in (3, 4):
-                    group_v(1, k - 3, CFG["gv"][k - 1])
-                if k in (3, 5) and CFG["t5"][2 * sb - 1] == "V":
-                    regroup_y(sb - 1, 1, "V")
-                if k == 4:
-                    quant_y(0, 1)
-                    store_codes(0, 1)
-                    store_scales(0, 0, 1024)
+                for u in queue[k - 1 : k]:
+                    unit_early(u)
+                inner(k, engine="S" if k in CFG["innerS"] else "V")
+                if k == 1:
+                    quant_v(0, 1, 0, 256, 0)
+                    quant_v(0, 1, 256, GC, 0)
+                    quant_v(0, 1, GC, 512, GC)
+                else:
+                    unit_quant(queue[k - 2])
+                unit_main(queue[k - 1])
                 outer(k)
                 quant_gated(k, 0)
-                if k == 1:
-                    quant_v(0, 1)
                 if k in (2, 4):
                     quant_x(sb + 1)
-                if k in (4, 5):
-                    quant_v(1, k - 4)
-                if k in (3, 5):
-                    quant_y(sb - 1, 0)
-                    store_codes(sb - 1, 0)
                 for q in range(4 * k + 8, 4 * k + 12):
                     logits(q)
                 if jg == 1:
@@ -419,52 +446,51 @@ def tile_contextpriorintrainteraggregation_x2_kernel(
             for t in range(4):
                 scale_y(2, 0, t, "S")
             store_y(2, 0)
+            unit_early(("y", 1, 1))
             for t in range(4):
                 for j in range(2):
                     aggregate_pass(2, 1, t, j)
                 scale_y(2, 1, t, "S")
             store_y(2, 1)
-            if CFG["t5"][4] != "V":
-                regroup_y(2, 0, CFG["t5"][4])
+            unit_early(("y", 2, 0))
             inner(6)
             gate(7)
             quant_gated(6, 0)
             inner(7)
-            if CFG["t5"][4] == "V":
-                regroup_y(2, 0, "V")
-            quant_y(1, 1)
-            store_codes(1, 1)
-            store_scales(1, 0, 1024)
+            unit_quant(("y", 1, 0))
             quant_gated(7, 0)
+            unit_main(("y", 1, 1))
             outer(6)
             for t in range(4):
                 for j in range(2):
                     aggregate_pass(3, 0, t, j)
                 scale_y(3, 0, t, "S")
             store_y(3, 0)
-            if CFG["t5"][5] != "V":
-                regroup_y(2, 1, CFG["t5"][5])
+            unit_early(("y", 2, 1))
+            unit_quant(("y", 1, 1))
+            unit_main(("y", 2, 0))
             outer(7)
             quant_gated(6, 1)
-            if CFG["t5"][5] == "V":
-                regroup_y(2, 1, "V")
             quant_gated(7, 1)
-            for t in range(4):
+            for t in range(3):
                 aggregate_pass(3, 1, t, 0)
-            for t in range(4):
+            for t in range(3):
                 aggregate_pass(3, 1, t, 1)
-            regroup_y(3, 0, CFG["t5"][6])
-            quant_y(2, 0)
-            store_codes(2, 0)
-            for t in range(4):
+            unit_quant(("y", 2, 0))
+            unit_main(("y", 2, 1))
+            unit_main(("y", 3, 0))
+            unit_early(("y", 3, 0))
+            scale_y(3, 1, 0, CFG["yc"][0])
+            for j in range(2):
+                aggregate_pass(3, 1, 3, j)
+            for t in range(1, 4):
                 scale_y(3, 1, t, CFG["yc"][t])
             store_y(3, 1)
-            quant_y(2, 1)
-            store_codes(2, 1)
-            store_scales(2, 0, 1024)
-            quant_y(3, 0)
-            store_codes(3, 0)
-            regroup_y(3, 1, "X")
-            quant_y(3, 1)
+            unit_quant(("y", 2, 1))
+            unit_quant(("y", 3, 0))
+            regroup_y(3, 1, "S", 0, CFG["cut"])
+            regroup_y(3, 1, "V", CFG["cut"], 512)
+            quant_y(3, 1, 0, CFG["cut"], 0)
+            quant_y(3, 1, CFG["cut"], 512, CFG["cut"])
             store_codes(3, 1)
             store_scales(3, 0, 1024)

@@ -15,7 +15,7 @@ ACT = mybir.ActivationFunctionType
 
 B, N, C, E = 2, 1024, 512, 512
 P = 128
-CFG = {("v", 1, 0): "G", ("v", 1, 1): "G", ("y", 0, 0): "G", ("y", 0, 1): "G", ("y", 1, 0): "G", ("y", 1, 1): "G", ("y", 2, 0): "G", ("y", 2, 1): "S", ("y", 3, 0): "S", "innerS": [], "yc": ["S", "V", "V", "S"], "cut": 256}
+CFG = {("v", 1, 0): "G", ("v", 1, 1): "G", ("y", 0, 0): "S", ("y", 0, 1): "G", ("y", 1, 0): "G", ("y", 1, 1): "S", ("y", 2, 0): "G", ("y", 2, 1): "S", ("y", 3, 0): "V", "GC": 384, "icut": 384, "innerS": [4, 2], "yc": ["S", "S", "S", "S"], "cut": 256}
 FLOPS = 2 * B * N * N * C + 2 * 2 * B * N * N * E
 
 
@@ -31,7 +31,7 @@ def tile_contextpriorintrainteraggregation_x2_kernel(
         gated = ctx.enter_context(tc.tile_pool(name="gated", bufs=3))
         codes = ctx.enter_context(tc.tile_pool(name="codes", bufs=6))
         results = ctx.enter_context(tc.tile_pool(name="results", bufs=4))
-        regroups = ctx.enter_context(tc.tile_pool(name="regroups", bufs=2))
+        regroups = ctx.enter_context(tc.tile_pool(name="regroups", bufs=4))
         vgroups = ctx.enter_context(tc.tile_pool(name="vgroups", bufs=1))
         ggroups = ctx.enter_context(tc.tile_pool(name="ggroups", bufs=1))
         zbanks = ctx.enter_context(tc.psum_pool(name="zbanks", bufs=4))
@@ -71,11 +71,12 @@ def tile_contextpriorintrainteraggregation_x2_kernel(
         def load_x(sb, halves):
             n, gp = divmod(sb, 2)
             rows = x[n, 512 * gp : 512 * gp + 512, :].rearrange("(p t) k -> p t k", t=4)
-            x_raw = raws.tile([P, 4, C], BF16, name="x_raw")
-            x_tiles[sb] = x_raw
+            if sb not in x_tiles:
+                x_raw = raws.tile([P, 4, C], BF16, name="x_raw")
+                x_tiles[sb] = x_raw
             for half in halves:
                 lo, hi = half
-                nc.sync.dma_start(out=x_raw[:, lo:hi, :], in_=rows[:, lo:hi, :])
+                nc.sync.dma_start(out=x_tiles[sb][:, lo:hi, :], in_=rows[:, lo:hi, :])
 
         def load_v(n, jg):
             v_raw = raws.tile([P, 4, E], BF16, name="v_raw")
@@ -184,9 +185,9 @@ def tile_contextpriorintrainteraggregation_x2_kernel(
                 scale=1.0,
             )
 
-        def gate(k, c0=0, c1=512):
+        def gate(k, c0=0, c1=512, s0=0, s1=4):
             jg = k % 2
-            for s in range(4):
+            for s in range(s0, s1):
                 pg = p_tiles[k][:, s, c0:c1]
                 nc.vector.tensor_scalar(
                     out=pg, in0=pg, scalar1=bg_col[:, 8 * jg + 2 * s + 1 : 8 * jg + 2 * s + 2], scalar2=None, op0=ALU.mult
@@ -218,14 +219,16 @@ def tile_contextpriorintrainteraggregation_x2_kernel(
                 op=ALU.subtract,
             )
 
-        def quant_gated(k, h):
-            g_codes = codes.tile([P, 512], U32, name="g_codes", align_bytes=64)
-            g_plane = codes.tile([P, 512], U8, name="g_plane", align_bytes=64)
-            code_tiles[k // 2, h, k % 2] = (g_codes, g_plane)
+        def quant_gated(k, h, c0=0, c1=512):
+            if c0 == 0:
+                g_codes = codes.tile([P, 512], U32, name="g_codes", align_bytes=64)
+                g_plane = codes.tile([P, 512], U8, name="g_plane", align_bytes=64)
+                code_tiles[k // 2, h, k % 2] = (g_codes, g_plane)
+            g_codes, g_plane = code_tiles[k // 2, h, k % 2]
             nc.vector.quantize_mx(
-                out=g_codes[:].bitcast(FP8X4),
-                scales=g_plane[:],
-                in_=gated_tiles[k, h][:].rearrange("p c s -> p (c s)"),
+                out=g_codes[:, c0:c1].bitcast(FP8X4),
+                scales=g_plane[:, c0:c1],
+                in_=gated_tiles[k, h][:, c0:c1, :].rearrange("p c s -> p (c s)"),
             )
 
         def aggregate_pass(sb, h, t, jg):
@@ -255,10 +258,10 @@ def tile_contextpriorintrainteraggregation_x2_kernel(
             else:
                 nc.vector.tensor_scalar(out=dst, in0=src, scalar1=1.0 / 32.0, scalar2=None, op0=ALU.mult)
 
-        def store_y(sb, h):
+        def store_y(sb, h, t0=0, t1=4):
             n, gp = divmod(sb, 2)
             dst = out_0[n, 512 * gp : 512 * gp + 512, 512 * h : 512 * h + 512].rearrange("(p t) e -> p t e", t=4)
-            nc.sync.dma_start(out=dst, in_=result_tiles[sb, h][:])
+            nc.sync.dma_start(out=dst[:, t0:t1, :], in_=result_tiles[sb, h][:, t0:t1, :])
 
         def regroup_y(sb, h, engine, e0=0, e1=512):
             pool, what = (ggroups, "part_g") if engine == "G" else (regroups, "y_part%d" % (e1 - e0))
@@ -275,31 +278,31 @@ def tile_contextpriorintrainteraggregation_x2_kernel(
                 in_=y_groups[sb, h, base][:, e0 - base : e1 - base, :].rearrange("p c t -> p (c t)"),
             )
 
-        def store_codes(sb, h):
+        def store_codes(sb, h, e0=0, e1=512):
             n, gp = divmod(sb, 2)
             m0 = 1024 * n + 512 * h
             nc.sync.dma_start(
-                out=out_1[gp].rearrange("p m t -> p (m t)")[:, 4 * m0 : 4 * m0 + 2048].bitcast(I32),
-                in_=y_codes[:, gp, m0 : m0 + 512].bitcast(I32),
+                out=out_1[gp].rearrange("p m t -> p (m t)")[:, 4 * (m0 + e0) : 4 * (m0 + e1)].bitcast(I32),
+                in_=y_codes[:, gp, m0 + e0 : m0 + e1].bitcast(I32),
             )
 
-        def store_scales(sb, h, width):
+        def store_scales(sb, h, width, both=False):
             n, gp = divmod(sb, 2)
             m0 = 1024 * n + 512 * h
             for quad in range(4):
-                nc.sync.dma_start(
+                (nc.scalar if both else nc.sync).dma_start(
                     out=out_2[gp, 4 * quad : 4 * quad + 4, m0 : m0 + width].bitcast(I32),
                     in_=y_plane[32 * quad : 32 * quad + 4, gp, m0 : m0 + width].bitcast(I32),
                 )
 
-        GC = 384
+        GC = CFG["GC"]
 
         def unit_early(u):
             kind, a, d = u
             f = group_v if kind == "v" else regroup_y
             if CFG[u] == "S":
                 f(a, d, "S")
-            elif CFG[u] == "G":
+            elif CFG[u] in "GX":
                 f(a, d, "S", GC, 512)
 
         def unit_main(u):
@@ -307,15 +310,20 @@ def tile_contextpriorintrainteraggregation_x2_kernel(
             f = group_v if kind == "v" else regroup_y
             if CFG[u] == "V":
                 f(a, d, "V")
-            elif CFG[u] == "G":
+            elif CFG[u] in "GH":
                 f(a, d, "G", 0, GC)
+                if CFG[u] == "H":
+                    f(a, d, "V", GC, 512)
+            elif CFG[u] == "X":
+                f(a, d, "V", 0, GC)
 
         def unit_quant(u):
             kind, a, d = u
             f = quant_v if kind == "v" else quant_y
-            if CFG[u] in ("G", "T"):
+            if CFG[u] in "GHX":
                 f(a, d, 0, 256, 0)
-                f(a, d, 256, GC, 0)
+                if GC > 256:
+                    f(a, d, 256, GC, 0)
                 f(a, d, GC, 512, GC)
             else:
                 f(a, d)
@@ -343,7 +351,7 @@ def tile_contextpriorintrainteraggregation_x2_kernel(
                     out=w_raw[:, 1024 * jg : 1024 * jg + 1024].bitcast(I32),
                     in_=w_words[0, :, 1024 * jg : 1024 * jg + 1024].bitcast(I32),
                 )
-            load_x(0, ((0, 2), (2, 4)))
+                load_x(0, ((2 * jg, 2 * jg + 2),))
             load_v(0, 0)
             load_x(1, ((0, 4),))
             load_v(0, 1)
@@ -363,9 +371,10 @@ def tile_contextpriorintrainteraggregation_x2_kernel(
             nc.scalar.copy(out=bg_col[:], in_=bg_bank[:, 0:16])
             permute_w(0)
             permute_ws(0)
-            quant_x(0, 0, 256)
-            copy_x(0, 1, "S")
             permute_w(1)
+            quant_x(0, 0, 256)
+            copy_x(0, 1, "V")
+            permute_ws(1)
             quant_x(0, 256, 512)
             for c0 in (0, 256):
                 for q in range(4):
@@ -373,7 +382,6 @@ def tile_contextpriorintrainteraggregation_x2_kernel(
                 for q in range(4):
                     sigmoid(q, c0, c0 + 256)
             gate(0, 0, 256)
-            permute_ws(1)
             for q in range(4, 8):
                 logits(q)
                 sigmoid(q)
@@ -397,6 +405,9 @@ def tile_contextpriorintrainteraggregation_x2_kernel(
                 sb, jg = divmod(k, 2)
                 gate(k)
                 quant_gated(k - 1, 1)
+                if k in CFG["innerS"]:
+                    inner(k, 0, CFG["icut"], "V")
+                    inner(k, CFG["icut"], 512, "S")
                 if jg == 0:
                     for t in range(4):
                         scale_y(sb - 1, 0, t, "S")
@@ -420,10 +431,12 @@ def tile_contextpriorintrainteraggregation_x2_kernel(
                     copy_x(sb + 2, 1, "S")
                 for u in queue[k - 1 : k]:
                     unit_early(u)
-                inner(k, engine="S" if k in CFG["innerS"] else "V")
+                if k not in CFG["innerS"]:
+                    inner(k)
                 if k == 1:
                     quant_v(0, 1, 0, 256, 0)
-                    quant_v(0, 1, 256, GC, 0)
+                    if GC > 256:
+                        quant_v(0, 1, 256, GC, 0)
                     quant_v(0, 1, GC, 512, GC)
                 else:
                     unit_quant(queue[k - 2])
@@ -469,28 +482,34 @@ def tile_contextpriorintrainteraggregation_x2_kernel(
             unit_early(("y", 2, 1))
             unit_quant(("y", 1, 1))
             unit_main(("y", 2, 0))
-            outer(7)
+            outer(7, 0, 256)
             quant_gated(6, 1)
-            quant_gated(7, 1)
-            for t in range(3):
-                aggregate_pass(3, 1, t, 0)
-            for t in range(3):
-                aggregate_pass(3, 1, t, 1)
+            quant_gated(7, 1, 0, 256)
+            for t in range(2):
+                for j in range(2):
+                    aggregate_pass(3, 1, t, j)
+            outer(7, 256, 512)
+            aggregate_pass(3, 1, 2, 0)
             unit_quant(("y", 2, 0))
-            unit_main(("y", 2, 1))
-            unit_main(("y", 3, 0))
-            unit_early(("y", 3, 0))
             scale_y(3, 1, 0, CFG["yc"][0])
+            scale_y(3, 1, 1, CFG["yc"][1])
+            store_y(3, 1, 0, 2)
+            quant_gated(7, 1, 256, 512)
+            aggregate_pass(3, 1, 2, 1)
             for j in range(2):
                 aggregate_pass(3, 1, 3, j)
-            for t in range(1, 4):
-                scale_y(3, 1, t, CFG["yc"][t])
-            store_y(3, 1)
+            unit_main(("y", 2, 1))
             unit_quant(("y", 2, 1))
+            unit_main(("y", 3, 0))
+            unit_early(("y", 3, 0))
+            for t in range(2, 4):
+                scale_y(3, 1, t, CFG["yc"][t])
+            store_y(3, 1, 2, 4)
             unit_quant(("y", 3, 0))
             regroup_y(3, 1, "S", 0, CFG["cut"])
             regroup_y(3, 1, "V", CFG["cut"], 512)
-            quant_y(3, 1, 0, CFG["cut"], 0)
             quant_y(3, 1, CFG["cut"], 512, CFG["cut"])
-            store_codes(3, 1)
-            store_scales(3, 0, 1024)
+            store_codes(3, 1, CFG["cut"], 512)
+            quant_y(3, 1, 0, CFG["cut"], 0)
+            store_codes(3, 1, 0, CFG["cut"])
+            store_scales(3, 0, 1024, True)

from contextlib import ExitStack

import concourse.mybir as mybir
from concourse.masks import make_identity

F32 = mybir.dt.float32
BF16 = mybir.dt.bfloat16
U32 = mybir.dt.uint32
I32 = mybir.dt.int32
U8 = mybir.dt.uint8
FP8X4 = mybir.dt.float8_e4m3fn_x4
FP4X4 = mybir.dt.float4_e2m1fn_x4
ALU = mybir.AluOpType
ACT = mybir.ActivationFunctionType

B, N, C, E = 2, 1024, 512, 512
P = 128
CFG = {("v", 1, 0): "G", ("v", 1, 1): "G", ("y", 0, 0): "S", ("y", 0, 1): "G", ("y", 1, 0): "G", ("y", 1, 1): "S", ("y", 2, 0): "G", ("y", 2, 1): "S", ("y", 3, 0): "V", "GC": 384, "icut": 384, "innerS": [4, 2], "yc": ["S", "S", "S", "S"], "cut": 256}
FLOPS = 2 * B * N * N * C + 2 * 2 * B * N * N * E


def tile_contextpriorintrainteraggregation_x2_kernel(
    tc, x, w_words, w_scales, b, g, v, out_0, out_1, out_2
):
    nc = tc.nc
    with ExitStack() as ctx:
        keep = ctx.enter_context(tc.tile_pool(name="keep", bufs=1))
        raws = ctx.enter_context(tc.tile_pool(name="raws", bufs=4))
        grouped = ctx.enter_context(tc.tile_pool(name="grouped", bufs=2))
        priors = ctx.enter_context(tc.tile_pool(name="priors", bufs=4))
        gated = ctx.enter_context(tc.tile_pool(name="gated", bufs=3))
        codes = ctx.enter_context(tc.tile_pool(name="codes", bufs=6))
        results = ctx.enter_context(tc.tile_pool(name="results", bufs=4))
        regroups = ctx.enter_context(tc.tile_pool(name="regroups", bufs=4))
        vgroups = ctx.enter_context(tc.tile_pool(name="vgroups", bufs=1))
        ggroups = ctx.enter_context(tc.tile_pool(name="ggroups", bufs=1))
        zbanks = ctx.enter_context(tc.psum_pool(name="zbanks", bufs=4))
        ybanks = ctx.enter_context(tc.psum_pool(name="ybanks", bufs=3))
        cbank = ctx.enter_context(tc.psum_pool(name="cbank", bufs=1))

        w_raw = keep.tile([P, 2 * N], U8, name="w_raw", align_bytes=64)
        ws_raw = keep.tile([P, N], U8, name="ws_raw", align_bytes=64)
        w_codes = [keep.tile([P, 4, P, 2], U8, name="w_codes%d" % i, align_bytes=64) for i in range(2)]
        w_plane = [keep.tile([P, 4, P], U8, name="w_plane%d" % i, align_bytes=64) for i in range(2)]
        bg_rows = keep.tile([P, N], BF16, name="bg_rows", align_bytes=64)
        bg_col = keep.tile([P, 16], F32, name="bg_col")
        bg_bank = cbank.tile([P, 16 + P], BF16, name="bg_bank")
        ident_b = keep.tile([P, P], BF16, name="ident_b")
        ident = keep.tile([P, P], F32, name="ident")
        warm = keep.tile([P, 1], F32, name="warm")
        warm2 = keep.tile([P, 1], F32, name="warm2")
        x_codes = [keep.tile([P, 512], U32, name="x_codes%d" % i, align_bytes=64) for i in range(4)]
        x_plane = [keep.tile([P, 512], U8, name="x_plane%d" % i, align_bytes=64) for i in range(4)]
        v_codes = [keep.tile([P, 512], U32, name="v_codes%d" % i, align_bytes=64) for i in range(4)]
        v_plane = [keep.tile([P, 512], U8, name="v_plane%d" % i, align_bytes=64) for i in range(4)]
        y_codes = keep.tile([P, 2, 2 * N], U32, name="y_codes", align_bytes=64)
        y_plane = keep.tile([P, 2, 2 * N], U8, name="y_plane", align_bytes=64)

        x_tiles = {}
        v_tiles = {}
        x_groups = {}
        v_groups = {}
        p_tiles = {}
        z_tiles = {}
        gated_tiles = {}
        code_tiles = {}
        y_tiles = {}
        result_tiles = {}
        y_groups = {}

        def load_x(sb, halves):
            n, gp = divmod(sb, 2)
            rows = x[n, 512 * gp : 512 * gp + 512, :].rearrange("(p t) k -> p t k", t=4)
            if sb not in x_tiles:
                x_raw = raws.tile([P, 4, C], BF16, name="x_raw")
                x_tiles[sb] = x_raw
            for half in halves:
                lo, hi = half
                nc.sync.dma_start(out=x_tiles[sb][:, lo:hi, :], in_=rows[:, lo:hi, :])

        def load_v(n, jg):
            v_raw = raws.tile([P, 4, E], BF16, name="v_raw")
            v_tiles[n, jg] = v_raw
            nc.sync.dma_start(
                out=v_raw[:], in_=v[n, 512 * jg : 512 * jg + 512, :].rearrange("(p s) e -> p s e", s=4)
            )

        def permute_w(jg):
            nc.vector.tensor_copy(
                out=w_codes[jg][:],
                in_=w_raw[:, 1024 * jg : 1024 * jg + 1024].rearrange("p (m s b) -> p s m b", s=4, b=2),
            )

        def permute_ws(jg):
            nc.vector.tensor_copy(
                out=w_plane[jg][:],
                in_=ws_raw[:, 512 * jg : 512 * jg + 512].rearrange("p (m s) -> p s m", s=4),
            )

        def turn_x(sb, half):
            turned = zbanks.tile([P, 2, 2, P], F32, name="turned", tag="z")
            z_tiles["x", sb, half] = turned
            for i in range(2):
                words = x_tiles[sb][:, 2 * half + i, :].bitcast(F32)
                for u in range(2):
                    nc.tensor.transpose(turned[:, i, u, :], words[:, u : 256 : 2], ident[:])

        def copy_x(sb, half, engine):
            if half == 0:
                x_group = grouped.tile([P, 512, 4], BF16, name="x_group", align_bytes=64)
                x_groups[sb] = x_group
            dst = x_groups[sb][:, 256 * half : 256 * half + 256, :].rearrange("p c j -> p (c j)").bitcast(F32)
            dst = dst.rearrange("p (t r u) -> p t r u", t=2, u=2)
            src = z_tiles["x", sb, half][:].rearrange("p t u r -> p t r u")
            if engine == "S":
                nc.scalar.copy(out=dst, in_=src)
            else:
                nc.vector.tensor_copy(out=dst, in_=src)

        def quant_x(sb, c0=0, c1=512):
            nc.vector.quantize_mx(
                out=x_codes[sb][:, c0:c1].bitcast(FP8X4),
                scales=x_plane[sb][:, c0:c1],
                in_=x_groups[sb][:, c0:c1, :].rearrange("p c j -> p (c j)"),
            )

        def group_v(n, jg, engine, e0=0, e1=512, held=False):
            pool, what = (ggroups, "part_g") if engine == "G" or held else (grouped, "v_part%d" % (e1 - e0))
            v_part = pool.tile([P, e1 - e0, 4], BF16, name=what, align_bytes=64)
            v_groups[n, jg, e0] = v_part
            regroup(v_part[:], v_tiles[n, jg][:, :, e0:e1], engine)

        def regroup(part, rows, engine):
            dst = part.rearrange("p (c i) t -> p c t i", i=4)
            src = rows.rearrange("p t (c i) -> p c t i", i=4)
            if engine == "S":
                nc.scalar.copy(out=dst, in_=src)
            elif engine == "V":
                nc.vector.tensor_copy(out=dst, in_=src)
            else:
                nc.gpsimd.tensor_scalar(
                    out=part, in0=rows.rearrange("p t c -> p c t"), scalar1=1.0, scalar2=0.0, op0=ALU.mult, op1=ALU.add
                )

        def quant_v(n, jg, e0=0, e1=512, base=0):
            nc.vector.quantize_mx(
                out=v_codes[2 * n + jg][:, e0:e1].bitcast(FP8X4),
                scales=v_plane[2 * n + jg][:, e0:e1],
                in_=v_groups[n, jg, base][:, e0 - base : e1 - base, :].rearrange("p c s -> p (c s)"),
            )

        def logits(q, c0=0, c1=512):
            k, s = divmod(q, 4)
            sb, jg = divmod(k, 2)
            if c1 - c0 == 512 or s % 2 == 0:
                z = zbanks.tile([P, 512], F32, name="z", tag="z")
                z_tiles[q, c0] = z
                lo = 0
            else:
                z = z_tiles[q - 1, c0]
                z_tiles[q, c0] = z
                lo = 256
            nc.tensor.matmul_mx(
                out=z[:, lo : lo + c1 - c0],
                lhsT=w_codes[jg][:].rearrange("p s m b -> p (s m b)")[:, 256 * s : 256 * s + 256].bitcast(FP4X4),
                lhsT_scale=w_plane[jg][:, s, :],
                rhs=x_codes[sb][:, c0:c1].bitcast(FP8X4),
                rhs_scale=x_plane[sb][:, c0:c1],
                start=True,
                stop=True,
            )

        def sigmoid(q, c0=0, c1=512):
            k, s = divmod(q, 4)
            jg = k % 2
            if s == 0 and c0 == 0:
                prior = priors.tile([P, 4, 512], F32, name="prior")
                p_tiles[k] = prior
            lo = 256 * (s % 2) if c1 - c0 == 256 else 0
            nc.scalar.activation(
                out=p_tiles[k][:, s, c0:c1],
                in_=z_tiles[q, c0][:, lo : lo + c1 - c0],
                func=ACT.Sigmoid,
                bias=bg_col[:, 8 * jg + 2 * s : 8 * jg + 2 * s + 1],
                scale=1.0,
            )

        def gate(k, c0=0, c1=512, s0=0, s1=4):
            jg = k % 2
            for s in range(s0, s1):
                pg = p_tiles[k][:, s, c0:c1]
                nc.vector.tensor_scalar(
                    out=pg, in0=pg, scalar1=bg_col[:, 8 * jg + 2 * s + 1 : 8 * jg + 2 * s + 2], scalar2=None, op0=ALU.mult
                )

        def gated_tile(k, h, c0):
            if c0 == 0:
                gate_out = gated.tile([P, 512, 4], BF16, name="gate_out", align_bytes=64)
                gated_tiles[k, h] = gate_out
            return gated_tiles[k, h]

        def inner(k, c0=0, c1=512, engine="V"):
            dst = gated_tile(k, 0, c0)[:, c0:c1, :].rearrange("p (c i) s -> p c s i", i=4)
            src = p_tiles[k][:, :, c0:c1].rearrange("p s (c i) -> p c s i", i=4)
            if engine == "S":
                nc.scalar.copy(out=dst, in_=src)
            else:
                nc.vector.tensor_copy(out=dst, in_=src)

        def outer(k, c0=0, c1=512):
            jg = k % 2
            nc.vector.tensor_tensor(
                out=gated_tile(k, 1, c0)[:, c0:c1, :].rearrange("p (c i) s -> p c s i", i=4),
                in0=bg_bank[:, 8 * jg + 1 : 8 * jg + 8 : 2]
                .unsqueeze(1)
                .unsqueeze(3)
                .to_broadcast([P, (c1 - c0) // 4, 4, 4]),
                in1=p_tiles[k][:, :, c0:c1].rearrange("p s (c i) -> p c s i", i=4),
                op=ALU.subtract,
            )

        def quant_gated(k, h, c0=0, c1=512):
            if c0 == 0:
                g_codes = codes.tile([P, 512], U32, name="g_codes", align_bytes=64)
                g_plane = codes.tile([P, 512], U8, name="g_plane", align_bytes=64)
                code_tiles[k // 2, h, k % 2] = (g_codes, g_plane)
            g_codes, g_plane = code_tiles[k // 2, h, k % 2]
            nc.vector.quantize_mx(
                out=g_codes[:, c0:c1].bitcast(FP8X4),
                scales=g_plane[:, c0:c1],
                in_=gated_tiles[k, h][:, c0:c1, :].rearrange("p c s -> p (c s)"),
            )

        def aggregate_pass(sb, h, t, jg):
            n = sb // 2
            if jg == 0:
                y = ybanks.tile([P, 512], F32, name="y", tag="y")
                y_tiles[sb, h, t] = y
            g_codes, g_plane = code_tiles[sb, h, jg]
            nc.tensor.matmul_mx(
                out=y_tiles[sb, h, t][:],
                lhsT=g_codes[:, 128 * t : 128 * t + 128].bitcast(FP8X4),
                lhsT_scale=g_plane[:, 128 * t : 128 * t + 128],
                rhs=v_codes[2 * n + jg][:].bitcast(FP8X4),
                rhs_scale=v_plane[2 * n + jg][:],
                start=(jg == 0),
                stop=(jg == 1),
            )

        def scale_y(sb, h, t, engine):
            if (sb, h) not in result_tiles:
                result = results.tile([P, 4, 512], F32, name="result")
                result_tiles[sb, h] = result
            dst = result_tiles[sb, h][:, t, :]
            src = y_tiles[sb, h, t][:]
            if engine == "S":
                nc.scalar.activation(out=dst, in_=src, func=ACT.Copy, scale=1.0 / 32.0)
            else:
                nc.vector.tensor_scalar(out=dst, in0=src, scalar1=1.0 / 32.0, scalar2=None, op0=ALU.mult)

        def store_y(sb, h, t0=0, t1=4):
            n, gp = divmod(sb, 2)
            dst = out_0[n, 512 * gp : 512 * gp + 512, 512 * h : 512 * h + 512].rearrange("(p t) e -> p t e", t=4)
            nc.sync.dma_start(out=dst[:, t0:t1, :], in_=result_tiles[sb, h][:, t0:t1, :])

        def regroup_y(sb, h, engine, e0=0, e1=512):
            pool, what = (ggroups, "part_g") if engine == "G" else (regroups, "y_part%d" % (e1 - e0))
            y_part = pool.tile([P, e1 - e0, 4], BF16, name=what, align_bytes=64)
            y_groups[sb, h, e0] = y_part
            regroup(y_part[:], result_tiles[sb, h][:, :, e0:e1], engine)

        def quant_y(sb, h, e0=0, e1=512, base=0):
            n, gp = divmod(sb, 2)
            m0 = 1024 * n + 512 * h
            nc.vector.quantize_mx(
                out=y_codes[:, gp, m0 + e0 : m0 + e1].bitcast(FP8X4),
                scales=y_plane[:, gp, m0 + e0 : m0 + e1],
                in_=y_groups[sb, h, base][:, e0 - base : e1 - base, :].rearrange("p c t -> p (c t)"),
            )

        def store_codes(sb, h, e0=0, e1=512):
            n, gp = divmod(sb, 2)
            m0 = 1024 * n + 512 * h
            nc.sync.dma_start(
                out=out_1[gp].rearrange("p m t -> p (m t)")[:, 4 * (m0 + e0) : 4 * (m0 + e1)].bitcast(I32),
                in_=y_codes[:, gp, m0 + e0 : m0 + e1].bitcast(I32),
            )

        def store_scales(sb, h, width, both=False):
            n, gp = divmod(sb, 2)
            m0 = 1024 * n + 512 * h
            for quad in range(4):
                (nc.scalar if both else nc.sync).dma_start(
                    out=out_2[gp, 4 * quad : 4 * quad + 4, m0 : m0 + width].bitcast(I32),
                    in_=y_plane[32 * quad : 32 * quad + 4, gp, m0 : m0 + width].bitcast(I32),
                )

        GC = CFG["GC"]

        def unit_early(u):
            kind, a, d = u
            f = group_v if kind == "v" else regroup_y
            if CFG[u] == "S":
                f(a, d, "S")
            elif CFG[u] in "GX":
                f(a, d, "S", GC, 512)

        def unit_main(u):
            kind, a, d = u
            f = group_v if kind == "v" else regroup_y
            if CFG[u] == "V":
                f(a, d, "V")
            elif CFG[u] in "GH":
                f(a, d, "G", 0, GC)
                if CFG[u] == "H":
                    f(a, d, "V", GC, 512)
            elif CFG[u] == "X":
                f(a, d, "V", 0, GC)

        def unit_quant(u):
            kind, a, d = u
            f = quant_v if kind == "v" else quant_y
            if CFG[u] in "GHX":
                f(a, d, 0, 256, 0)
                if GC > 256:
                    f(a, d, 256, GC, 0)
                f(a, d, GC, 512, GC)
            else:
                f(a, d)
            if kind == "y":
                store_codes(a, d)
                if d == 1:
                    store_scales(a, 0, 1024)

        with tc.manual_schedule():
            nc.vector.memset(bg_rows[:].bitcast(I32), 0)
            nc.gpsimd.memset(ws_raw[:].bitcast(I32), 0)
            make_identity(nc, ident_b[:])
            make_identity(nc, ident[:])
            nc.gpsimd.memset(warm[:], 0.0)
            nc.scalar.dma_start(out=bg_rows[0:1, :], in_=b.unsqueeze(0))
            nc.scalar.dma_start(out=bg_rows[1:2, :], in_=g.unsqueeze(0))
            for quad in range(4):
                nc.scalar.dma_start(
                    out=ws_raw[32 * quad : 32 * quad + 4, :].bitcast(I32),
                    in_=w_scales[0, 4 * quad : 4 * quad + 4, :].bitcast(I32),
                )
            nc.scalar.activation(out=warm2[:], in_=warm[:], func=ACT.Sigmoid)
            for jg in range(2):
                nc.sync.dma_start(
                    out=w_raw[:, 1024 * jg : 1024 * jg + 1024].bitcast(I32),
                    in_=w_words[0, :, 1024 * jg : 1024 * jg + 1024].bitcast(I32),
                )
                load_x(0, ((2 * jg, 2 * jg + 2),))
            load_v(0, 0)
            load_x(1, ((0, 4),))
            load_v(0, 1)
            load_x(2, ((0, 4),))
            load_x(3, ((0, 4),))
            load_v(1, 0)
            load_v(1, 1)

            turn_x(0, 0)
            for i in range(8):
                jg, s = divmod(i, 4)
                nc.tensor.transpose(
                    bg_bank[:, 2 * i : 2 * i + P], bg_rows[:, 512 * jg + s : 512 * jg + 512 : 4], ident_b[:]
                )
            turn_x(0, 1)
            copy_x(0, 0, "S")
            nc.scalar.copy(out=bg_col[:], in_=bg_bank[:, 0:16])
            permute_w(0)
            permute_ws(0)
            permute_w(1)
            quant_x(0, 0, 256)
            copy_x(0, 1, "V")
            permute_ws(1)
            quant_x(0, 256, 512)
            for c0 in (0, 256):
                for q in range(4):
                    logits(q, c0, c0 + 256)
                for q in range(4):
                    sigmoid(q, c0, c0 + 256)
            gate(0, 0, 256)
            for q in range(4, 8):
                logits(q)
                sigmoid(q)
            turn_x(1, 0)
            turn_x(1, 1)
            copy_x(1, 0, "S")
            copy_x(1, 1, "S")
            group_v(0, 0, "S")
            inner(0, 0, 256)
            gate(0, 256, 512)
            inner(0, 256, 512)
            outer(0, 0, 256)
            outer(0, 256, 512)
            quant_gated(0, 0)
            quant_x(1)

            queue = [("v", 1, 0), ("v", 1, 1), ("y", 0, 0), ("y", 0, 1), ("y", 1, 0)]
            for q in range(8, 12):
                logits(q)
            for k in range(1, 6):
                sb, jg = divmod(k, 2)
                gate(k)
                quant_gated(k - 1, 1)
                if k in CFG["innerS"]:
                    inner(k, 0, CFG["icut"], "V")
                    inner(k, CFG["icut"], 512, "S")
                if jg == 0:
                    for t in range(4):
                        scale_y(sb - 1, 0, t, "S")
                    store_y(sb - 1, 0)
                if k == 1:
                    group_v(0, 1, "S", 0, GC, True)
                    group_v(0, 1, "S", GC, 512)
                    quant_v(0, 0)
                for q in range(4 * k + 4, 4 * k + 8):
                    sigmoid(q)
                if jg == 0:
                    for t in range(4):
                        for j in range(2):
                            aggregate_pass(sb - 1, 1, t, j)
                        scale_y(sb - 1, 1, t, "S")
                    store_y(sb - 1, 1)
                if k in (1, 3):
                    turn_x(sb + 2, 0)
                    turn_x(sb + 2, 1)
                    copy_x(sb + 2, 0, "S")
                    copy_x(sb + 2, 1, "S")
                for u in queue[k - 1 : k]:
                    unit_early(u)
                if k not in CFG["innerS"]:
                    inner(k)
                if k == 1:
                    quant_v(0, 1, 0, 256, 0)
                    if GC > 256:
                        quant_v(0, 1, 256, GC, 0)
                    quant_v(0, 1, GC, 512, GC)
                else:
                    unit_quant(queue[k - 2])
                unit_main(queue[k - 1])
                outer(k)
                quant_gated(k, 0)
                if k in (2, 4):
                    quant_x(sb + 1)
                for q in range(4 * k + 8, 4 * k + 12):
                    logits(q)
                if jg == 1:
                    for t in range(4):
                        for j in range(2):
                            aggregate_pass(sb, 0, t, j)

            gate(6)
            quant_gated(5, 1)
            for q in range(28, 32):
                sigmoid(q)
            for t in range(4):
                scale_y(2, 0, t, "S")
            store_y(2, 0)
            unit_early(("y", 1, 1))
            for t in range(4):
                for j in range(2):
                    aggregate_pass(2, 1, t, j)
                scale_y(2, 1, t, "S")
            store_y(2, 1)
            unit_early(("y", 2, 0))
            inner(6)
            gate(7)
            quant_gated(6, 0)
            inner(7)
            unit_quant(("y", 1, 0))
            quant_gated(7, 0)
            unit_main(("y", 1, 1))
            outer(6)
            for t in range(4):
                for j in range(2):
                    aggregate_pass(3, 0, t, j)
                scale_y(3, 0, t, "S")
            store_y(3, 0)
            unit_early(("y", 2, 1))
            unit_quant(("y", 1, 1))
            unit_main(("y", 2, 0))
            outer(7, 0, 256)
            quant_gated(6, 1)
            quant_gated(7, 1, 0, 256)
            for t in range(2):
                for j in range(2):
                    aggregate_pass(3, 1, t, j)
            outer(7, 256, 512)
            aggregate_pass(3, 1, 2, 0)
            unit_quant(("y", 2, 0))
            scale_y(3, 1, 0, CFG["yc"][0])
            scale_y(3, 1, 1, CFG["yc"][1])
            store_y(3, 1, 0, 2)
            quant_gated(7, 1, 256, 512)
            aggregate_pass(3, 1, 2, 1)
            for j in range(2):
                aggregate_pass(3, 1, 3, j)
            unit_main(("y", 2, 1))
            unit_quant(("y", 2, 1))
            unit_main(("y", 3, 0))
            unit_early(("y", 3, 0))
            for t in range(2, 4):
                scale_y(3, 1, t, CFG["yc"][t])
            store_y(3, 1, 2, 4)
            unit_quant(("y", 3, 0))
            regroup_y(3, 1, "S", 0, CFG["cut"])
            regroup_y(3, 1, "V", CFG["cut"], 512)
            quant_y(3, 1, CFG["cut"], 512, CFG["cut"])
            store_codes(3, 1, CFG["cut"], 512)
            quant_y(3, 1, 0, CFG["cut"], 0)
            store_codes(3, 1, 0, CFG["cut"])
            store_scales(3, 0, 1024, True)
